import numpy as np, ml_dtypes
CORES = [6,15,38,47]
N = 4
import mx_ref
BF = ml_dtypes.bfloat16
def gentries(a):
    return np.ascontiguousarray(a.reshape(8, 16, -1).transpose(0, 2, 1)).reshape(8, -1)
def gtable(e):
    e = np.asarray(e); return np.ascontiguousarray(e.reshape(8, -1, 16).transpose(0, 2, 1)).reshape(128, -1).astype(np.int32)
def tile(rs):
    return np.stack(rs, axis=2).reshape(128, -1).astype(BF)
def pick(q, e):
    c = np.concatenate([q[0].reshape(128, -1, 4), np.zeros((128, 1, 4), np.uint8)], axis=1); s = np.concatenate([q[1], np.ones((16, 1), np.uint8)], axis=1)
    return (np.ascontiguousarray(c[:, e].reshape(128, -1)), np.ascontiguousarray(s[:, e]))
def join(*qs):
    return (np.concatenate([q[0] for q in qs], axis=1), np.concatenate([q[1] for q in qs], axis=1))
def put(q, e, v):
    c, s = q[0].reshape(128, -1, 4).copy(), q[1].copy(); c[:, e] = v[0].reshape(128, -1, 4); s[:, e] = v[1]
    return (c.reshape(128, -1), s)
def pk(c, s):
    return (np.ascontiguousarray(c), mx_ref.live(s))
def emit(q):
    return q[0], q[1]
def packed(v, rng):
    q = [mx_ref.quantize(np.ascontiguousarray(v[r])) for r in range(N)]
    return np.stack([a for a, b in q]), np.stack([mx_ref.plane(b, rng) for a, b in q])
def values_of_codes():
    e, c = np.zeros((128, 128, 4), np.float32), np.zeros((128, 2, 4), np.uint8)
    e[np.arange(128), np.arange(128), 0] = 1
    c[:127, :, 0] = np.arange(256).reshape(2, 128).T[:127]
    return mx_ref.matmul(mx_ref.quantize(e.reshape(128, 512).astype(BF)), (c.reshape(128, 8), np.full((16, 2), 127, np.uint8))).T.reshape(-1).astype(np.float64)
CODE_VALUE, SCALE_VALUE = values_of_codes(), 2.0 ** (np.arange(256) - 127.0)
def decode(q):
    return (CODE_VALUE[q[0]].reshape(16, 8, -1, 4) * SCALE_VALUE[q[1]][:, None, :, None] + 0.0).reshape(128, -1).astype(np.float32)
def f(rng, *shape):
    return mx_ref.flush((rng.standard_normal(shape, dtype=np.float32) * np.exp2(rng.integers(-2, 3, shape[:-1] + (1,)))).astype(BF))
def wide(rng, *shape, cols=0):
    v = rng.standard_normal(shape, dtype=np.float32) * np.exp2(rng.integers(-12, 13, shape)).astype(np.float32)
    if cols: v *= np.repeat(np.exp2(rng.integers(-cols, cols + 1, shape[:-2] + (1, shape[-1] // 4))) * (rng.random(shape[:-2] + (1, shape[-1] // 4)) > 0.0625), 4, axis=-1).astype(np.float32)
    return mx_ref.flush(v.astype(BF))
C, B, L, M, R = 320, 48, 416, 160, 3
MASK = [1, 2, 3]
def big(v):
    v = v.astype(np.float32)
    v[np.abs(v) < np.float32(2.0 ** -16)] = 0
    return v.astype(BF)
def numbers_of(rng):
    return {"x": big(f(rng, N, 128, 4 * C)), "u": np.array(f(rng, N, 128, 512)), "v": np.array(f(rng, N, 128, 512))}
def rings(rng, ends=False):
    p = [np.arange(C)[::1 - 2 * (h % 2)] if ends else rng.permutation(C) for h in range(8)]
    e = np.zeros((8, L), np.int64)
    for g in range(8):
        a, b = (g - 1) % 8, (g + 1) % 8
        e[g] = rng.permutation(np.concatenate([C * g + np.arange(C), C * a + p[a][:B], C * b + p[b][B:2 * B]]))
        if ends: e[g] = np.sort(e[g])[::1 - 2 * (g // 2 % 2)]
    return np.stack([gtable(e)] * N)
def layers(rng):
    return big(np.clip(f(rng, N, 128, 2048).astype(np.float32) * np.float32(0.25), -1.75, 1.75)).reshape(N, 8, 16, 4, 8, 16, 4)
def weights(rng, w):
    c, s = packed(np.ascontiguousarray(w).reshape(N, 128, 2048), rng)
    return {"wc": c, "ws": s}
def setup_inputs(rng):
    return {**numbers_of(rng), "ring": rings(rng), **weights(rng, layers(rng))}
def setup_inputs_ties(rng):
    d = numbers_of(rng)
    o = rng.permutation(N)
    same = rng.random((N, 8, C)) < rng.random((N, 8, 1))
    same[o[0]] = True
    same[o[0], rng.integers(8)] = False
    a = rng.integers(0, 3, (N, 8, C))
    b = np.where(same, a, rng.integers(0, 3, (N, 8, C)))
    least = max(257 if C > 256 else 0, 17 * C // 20) | 1
    for r in o[1:]:
        n = rng.permutation(np.arange(least, 19 * C // 20 + 1, 2))[:3]
        for i, g in enumerate(rng.permutation(8)[:3]):
            b[r, g] = a[r, g]
            j = rng.permutation(C)[:n[i]]
            more = rng.integers(1, 3, n[i])
            less = rng.integers(0, more)
            a[r, g, j] = more if o[r] % 2 else less
            b[r, g, j] = less if o[r] % 2 else more
    x = d["x"].reshape(N, 8, 16, C, 4)
    x[:, :, 0] = 0
    x[:, :, 0, :, 0] = a.astype(np.float32).astype(BF)
    x[:, :, 0, :, 1] = b.astype(np.float32).astype(BF)
    u = d["u"].reshape(N, 128, 128, 4)
    u[:, :, ::16] = 0
    for r in range(N):
        for h in range(0, 128, 16):
            u[r, h, h, 0] = 1.0 if o[r] % 2 else -1.0
            u[r, h, h, 1] = -1.0 if o[r] % 2 else 1.0
    w = layers(rng)
    w[:, :, :, :, :, 0] = 0
    return {"x": x.reshape(N, 128, 4 * C), "u": u.reshape(N, 128, 512), "v": d["v"], "ring": rings(rng), **weights(rng, w)}
def setup_inputs_near(rng):
    d = numbers_of(rng)
    o = rng.permutation(N) % 4
    k = rng.integers(0, 4, (N, 8, C))
    a = np.array([1.125, -1.125, 1.0, -1.0])[k]
    b = np.array([-1.25, 1.25, -1.125, 1.125])[k]
    x = d["x"].astype(np.float32).reshape(N, 8, 16, C, 4)
    x[:, :, :8] = 0
    u = d["u"].reshape(N, 128, 128, 4)
    u[:, :, ::16] = 0
    i = np.arange(32)
    s = np.exp2(-12.0 - i // 2 % 4)
    for r in range(N):
        z = 2.0 ** -30 if o[r] < 2 else 1.0
        x[r, :, 0, :, 0] = a[r] * z
        x[r, :, 1, :, 0] = b[r] * z
        for g in range(8):
            j = rng.permutation(C)[:32]
            x[r, g, 0, j, 0] = 0
            x[r, g, 1, j, 0] = 0
            x[r, g, 2, j, 0] = 1.96875
            x[r, g, 3, j, 0] = np.where(i % 2 == 0, 1.5, 1.125) * s
            x[r, g, 4, j, 0] = np.where(i % 2 == 0, -1.375, -1.0) * s
        for g in rng.permutation(8)[:4]:
            j = rng.integers(C)
            x[r, g, :8, j] = 0
            x[r, g, 0, j, 0] = 2.0 ** 14 * rng.choice([-1.0, 1.0])
        for h in range(0, 128, 16):
            z = 2.0 ** -30 if o[r] % 2 == 0 else 1.0
            u[r, h, h, 0] = 1.125 * z
            u[r, h + 1, h, 0] = z
            u[r, h + 3, h, 0] = z
            u[r, h + 4, h, 0] = z
    w = layers(rng)
    w[:, :, :8] = 0
    w[:, :, :, :, :, :8] = 0
    for g in range(8): w[:, g, 2, 0, g, 2, 0] = -0.5
    return {"x": x.reshape(N, 128, 4 * C).astype(BF), "u": u.reshape(N, 128, 512), "v": d["v"], "ring": rings(rng), **weights(rng, w)}
def setup_inputs_late(rng):
    d = numbers_of(rng)
    x = d["x"].astype(np.float32).reshape(N, 8, 16, C, 4)
    x[:, :, 0] = ((rng.permutation(N) % 2) * 0.25 - 0.125)[:, None, None, None]
    s = (N, 8, 8, C, 4)
    x[:, :, 8:] = rng.choice([-1.0, 1.0], s) * (1.0 + 0.125 * (2 * rng.integers(0, 4, s) + 1)) * np.exp2(10.0 - rng.integers(8, 15, s))
    x[:, :, 8, :, 0] = rng.choice([-1.0, 1.0], (N, 8, C)) * 1.96875 * 2.0 ** 10
    u = d["u"].reshape(N, 128, 128, 4)
    u[:, :, ::16] = 0
    for h in range(0, 128, 16): u[:, h, h, 0] = 1.0
    w = layers(rng)
    w[:, :, 8] = 0
    w[:, :, :, :, :, 8:] = (w[:, :, :, :, :, 8:].astype(np.float32) * np.float32(0.125)).astype(BF)
    w[:, :, :, 0, :, 8] = 0
    for g in range(8): w[:, g, 8, 0, g, 8, 0] = -0.5
    return {"x": x.reshape(N, 128, 4 * C).astype(BF), "u": u.reshape(N, 128, 512), "v": d["v"], "ring": rings(rng), **weights(rng, w)}
def setup_inputs_ends(rng):
    d = numbers_of(rng)
    o = rng.permutation(N)
    x = np.zeros((N, 8, 16, C, 4), np.float32)
    u = d["u"].reshape(N, 128, 128, 4)
    u[:, :, ::16] = 0
    v = rng.choice([-1.0, 1.0], (N, 128, 512)).astype(np.float32)
    w = np.zeros((N, 8, 16, 4, 8, 16, 4), np.float32)
    for r in range(N):
        i = o[r] % 4
        k = np.array([1.0, 1.0, 1.0, -1.0, -1.0, -1.0, 0.0, 0.0])[rng.permutation(8)]
        x[r, :, :8] = k[:, None, None, None] * (2.0 ** 14 if i % 2 == 0 else 2.0 ** -30)
        x[r, :, 8:] = 2.0 ** 14 * rng.choice([-1.0, 1.0], (1, 1, C, 1) if i < 2 else (8, 8, C, 4))
        z = 2.0 ** 30 if i // 2 == 0 else 2.0 ** -30
        s = rng.choice([-1.0, 1.0])
        for h in range(0, 128, 16): u[r, h:h + 8, h] = s * z
        v[r] *= np.float32(z)
        w[r, :, 8:, :, :, 8:] = 1.96875 if i == 0 else -1.96875 if i == 3 else (1.96875 if i == 1 else 2.0 ** -30) * rng.choice([-1.0, 1.0], (8, 8, 4, 8, 8, 4))
    return {"x": x.reshape(N, 128, 4 * C).astype(BF), "u": u.reshape(N, 128, 512), "v": v.astype(BF), "ring": rings(rng, True), **weights(rng, w.astype(BF))}
def setup_inputs_spread(rng):
    d = setup_inputs(rng)
    d["x"] = big(wide(rng, N, 128, 4 * C, cols=3).astype(np.float32) * np.float32(0.03125))
    return d
def check_inputs(d):
    b = []
    for k, most in (("x", 2.0 ** 14), ("u", 2.0 ** 30), ("v", 2.0 ** 30)):
        a = np.abs(d[k].astype(np.float32))
        if not (np.isfinite(a).all() and ((a == 0) | (a >= 2.0 ** -30) & (a <= most)).all()): b.append("a value of " + k)
    if (d["ring"] != d["ring"][:1]).any(): b.append("ring isn't the same on all ranks")
    e = gentries(d["ring"][0])
    if not ((e >= 0) & (e < 8 * C)).all(): b.append("an entry of ring")
    for g in range(8):
        h = e[g] // C
        if np.unique(e[g]).size != L: b.append("a place twice in a ring")
        if np.count_nonzero(h == g) != C or np.count_nonzero(h == (g - 1) % 8) != B or np.count_nonzero(h == (g + 1) % 8) != B: b.append("the groups of a ring's places")
    for k in range(2):
        if np.unique(e[k::2]).size != 4 * L: b.append("rings of equal parity share a place")
    none, least, most = [emit(mx_ref.quantize(np.full((128, 16), k, np.float32).astype(BF)))[1][0, 0] for k in (0.0, 2.0 ** -30, 1.96875)]
    for r in range(N):
        if ((d["wc"][r] == 0x7F) | (d["wc"][r] == 0xFF)).any(): b.append("wc: a code that is no number")
        s = mx_ref.live(d["ws"][r])
        if ((s != none) & ((s < least) | (s > most))).any(): b.append("ws: a scale out of range")
        elif (np.abs(decode(pk(d["wc"][r], d["ws"][r]))) > 2.0).any(): b.append("a number of W beyond 2 in size")
    return b
def turned(e, a):
    now = np.arange(8 * C)
    for first in (1, 0):
        new = now.copy()
        for g in range(first, 8, 2): new[np.roll(e[g], -a[g])] = now[e[g]]
        now = new
    return now.reshape(8, C)
def reference(x, u, v, ring, wc, ws):
    qu = [mx_ref.quantize(u[r]) for r in range(N)]
    lay = [pk(wc[r], ws[r]) for r in range(N)]
    now = [x[r] for r in range(N)]
    e = gentries(ring[0])
    ac = np.zeros((N, 8, R), np.float32)
    for t in range(R):
        own, sent = [], []
        for r in range(N):
            q = mx_ref.quantize(now[r])
            s = mx_ref.matmul(qu[r], q)
            a = np.count_nonzero(s[::16] > 0, axis=1)
            ac[r, :, t] = a
            p = turned(e, a)
            own.append(np.ascontiguousarray(decode(q).reshape(8, 16, C, 4)[p // C, :, p % C].transpose(0, 2, 1, 3)).reshape(128, 4 * C).astype(BF))
            sent.append(decode(mx_ref.quantize(np.ascontiguousarray(own[r][:, :4 * M]))).astype(BF))
        for r in range(N):
            z = np.concatenate([sent[r ^ MASK[t]], own[r][:, 4 * M:]], axis=1)
            q = mx_ref.quantize(z)
            now[r] = tile([mx_ref.matmul(pick(lay[r], np.arange(128 * b, 128 * b + 128)), q) * np.float32(0.03125) + z[:, b::4].astype(np.float32) for b in range(4)])
    y = np.zeros((N, 128, C), np.float32)
    oc, osc = np.zeros((N, 128, 4 * C), np.uint8), np.zeros((N, 16, C), np.uint8)
    for r in range(N):
        q = mx_ref.quantize(now[r])
        y[r] = mx_ref.matmul(mx_ref.quantize(v[r]), q)
        oc[r], osc[r] = emit(q)
    return {"y": y, "ac": ac, "oc": oc, "osc": osc}

@@ -1,0 +1,486 @@
+import numpy as np
+from concourse.mybir import dt, AluOpType, ActivationFunctionType
+
+N = 4
+MASKS = (1, 2, 3)
+NC, HALF, GRP, RING, DBL = 320, 160, 16, 416, 736
+CEN = 7 * NC
+WINC = 15 * NC
+IDB = 3 * DBL
+INV = WINC
+OP = AluOpType
+FN = ActivationFunctionType
+
+SCRATCH = {
+    "win": ("sbuf", [128, 4 * WINC], "bfloat16"),
+    "map": ("sbuf", [128, 2 * WINC], "float32"),
+    "src": ("sbuf", [128, IDB + WINC], "float32"),
+    "idt": ("sbuf", [128, 2560], "float32"),
+    "ivA": ("sbuf", [128, RING], "float32"), "ivB": ("sbuf", [128, RING], "float32"), "ivC": ("sbuf", [128, RING], "float32"),
+    "ri": ("sbuf", [128, 130], "int32"), "eu": ("sbuf", [128, 78], "uint16"), "xu": ("sbuf", [128, 130], "uint16"),
+    "su3": ("sbuf", [128, 60], "uint16"),
+    "pI": ("sbuf", [128, 8], "int32"), "gI": ("sbuf", [128, 8], "int32"), "pr": ("sbuf", [128, 8], "int32"), "p7": ("sbuf", [128, 8], "int32"),
+    "ul": ("sbuf", [128, 8], "uint16"),
+    "sc": ("sbuf", [128, 32], "float32"),
+    "jj": ("sbuf", [128, 48], "int32"), "cst": ("sbuf", [128, 48], "int32"), "mk": ("sbuf", [128, 48], "float32"), "kp8": ("sbuf", [128, 48], "float32"),
+    "ji": ("sbuf", [128, RING], "int32"), "mask": ("sbuf", [128, RING], "float32"), "keep": ("sbuf", [128, RING], "float32"),
+    "j20": ("sbuf", [128, 20], "float32"), "j832": ("sbuf", [128, 20], "float32"),
+    "hm0": ("sbuf", [128, RING], "float32"), "hs0": ("sbuf", [128, RING], "float32"),
+    "hm1": ("sbuf", [128, RING], "float32"), "hs1": ("sbuf", [128, RING], "float32"),
+    "bA": ("sbuf", [128, 72], "float32"), "mA": ("sbuf", [128, 72], "float32"), "mB": ("sbuf", [128, 72], "float32"),
+    "g1": ("sbuf", [128, 72], "float32"), "g2": ("sbuf", [128, 72], "float32"), "g3": ("sbuf", [128, 72], "float32"), "mC": ("sbuf", [128, 72], "float32"),
+    "pm": ("sbuf", [128, 40], "float32"), "lr": ("sbuf", [128, 40], "float32"),
+    "bt": ("sbuf", [128, 240], "float32"),
+    "bB": ("sbuf", [128, 20], "float32"), "mD": ("sbuf", [128, 20], "float32"), "mE": ("sbuf", [128, 20], "float32"), "thr": ("sbuf", [128, 20], "float32"),
+    "ta": ("sbuf", [128, 72], "float32"), "tb": ("sbuf", [128, 72], "float32"), "tc": ("sbuf", [128, 72], "float32"),
+    "td": ("sbuf", [128, 20], "float32"), "te": ("sbuf", [128, 20], "float32"), "tt": ("sbuf", [128, 20], "float32"), "tw": ("sbuf", [128, 20], "float32"),
+    "oA": ("sbuf", [128, 72], "uint16"), "oB": ("sbuf", [128, 20], "uint16"), "l4": ("sbuf", [128, 80], "uint16"),
+    "tab": ("sbuf", [128, 1152], "float32"),
+    "bm": ("sbuf", [128, 2 * HALF], "float32"), "bs": ("sbuf", [128, 2 * HALF], "float32"),
+    "cm": ("sbuf", [128, 48], "float32"), "cs": ("sbuf", [128, 48], "float32"), "acs": ("sbuf", [128, 4], "float32"),
+    "ew": ("sbuf", [128, 516], "bfloat16"), "e1": ("sbuf", [128, 516], "bfloat16"), "e32": ("sbuf", [128, 516], "bfloat16"),
+    "qe": ("sbuf", [128, 1024], "float8_e4m3fn_x4"), "se": ("sbuf", [128, 1024], "uint8"),
+    "ct": ("sbuf", [128, 512], "bfloat16"), "qc": ("sbuf", [128, 128], "float8_e4m3fn_x4"), "sct": ("sbuf", [128, 128], "uint8"),
+    "ft": ("sbuf", [128, 512], "bfloat16"), "qf": ("sbuf", [128, 128], "float8_e4m3fn_x4"), "sf": ("sbuf", [128, 128], "uint8"),
+    "ut": ("sbuf", [128, 512], "bfloat16"), "qu": ("sbuf", [128, 128], "float8_e4m3fn_x4"), "su": ("sbuf", [128, 128], "uint8"),
+    "qu2": ("sbuf", [128, 128], "float8_e4m3fn_x4"), "su2": ("sbuf", [128, 128], "uint8"),
+    "vt": ("sbuf", [128, 512], "bfloat16"), "qv": ("sbuf", [128, 128], "float8_e4m3fn_x4"), "sv": ("sbuf", [128, 128], "uint8"),
+    "wq": ("sbuf", [128, 512], "float8_e4m3fn_x4"), "wsb": ("sbuf", [128, 512], "uint8"),
+    "qx": ("sbuf", [128, NC], "float8_e4m3fn_x4"), "sx": ("sbuf", [128, NC], "uint8"),
+    "gr": ("sbuf", [128, 4 * HALF], "bfloat16"), "q1": ("sbuf", [128, HALF], "float8_e4m3fn_x4"), "s1": ("sbuf", [128, HALF], "uint8"),
+    "gt": ("sbuf", [128, 4 * HALF], "bfloat16"), "q2": ("sbuf", [128, HALF], "float8_e4m3fn_x4"), "s2": ("sbuf", [128, HALF], "uint8"),
+    "ow": ("sbuf", [128, 4 * HALF], "bfloat16"), "qo": ("sbuf", [128, HALF], "float8_e4m3fn_x4"), "so": ("sbuf", [128, HALF], "uint8"),
+    "zo": ("sbuf", [128, 4 * HALF], "bfloat16"), "zg": ("sbuf", [128, 4 * HALF], "bfloat16"),
+    "qzo": ("sbuf", [128, HALF], "float8_e4m3fn_x4"), "szo": ("sbuf", [128, HALF], "uint8"),
+    "qzg": ("sbuf", [128, HALF], "float8_e4m3fn_x4"), "szg": ("sbuf", [128, HALF], "uint8"),
+    "yt": ("sbuf", [128, NC], "float32"),
+}
+for _r in range(3):
+    SCRATCH["lc%d" % _r] = ("sbuf", [128, HALF], "float8_e4m3fn_x4")
+    SCRATCH["ls%d" % _r] = ("sbuf", [128, HALF], "uint8")
+for _b in range(8):
+    SCRATCH["ps%d" % _b] = ("psum", [128, 512], "float32")
+SEMAPHORES = ["cV", "cS", "cT", "cG", "dX", "dR", "dU", "dV", "dW", "shO", "shG", "dL", "dOut", "arr0", "arr1", "arr2", "sent"]
+
+
+def shifts(lo, hi):
+    out = []
+
+    def piece(p0, p1, q0):
+        slot = q0 // GRP - p0 // GRP + 7
+        out.append((p0, p1, q0, 4 * (NC * slot + lo), 4 * (hi - lo)))
+    for m in (1, 2):
+        k = GRP * m
+        piece(0, 128 - k, k)
+        piece(128 - k, 128, 0)
+        piece(k, 128, 0)
+        piece(0, k, 128 - k)
+    for grp in (1, 3, 5, 7):
+        for d in (3, -3):
+            piece(GRP * grp, GRP * grp + GRP, GRP * ((grp + d) % 8))
+    return out
+
+
+def rank_program(g, core, T, topo):
+    rank = T.rank_of(core)
+    if rank is None:
+        return
+    eng = {"V": g.vector, "S": g.scalar, "T": g.tensor, "G": g, "Y": g.sync}
+    own_sem = {"V": "cV", "S": "cS", "T": "cT", "G": "cG"}
+    total = {s: 0 for s in SEMAPHORES}
+    local = ("dX", "dR", "dU", "dV", "dW", "shO", "shG", "dL", "dOut")
+    known = {e: {} for e in eng}
+    writer, reader = {}, {}
+
+    def gate(e, r, w):
+        need = []
+        for t in r:
+            need += writer.get(t, [])
+        for t in w:
+            need += writer.get(t, [])
+            need += [x for x in reader.get(t, []) if x[3] != e]
+        best = {}
+        for sem, val, clk, _ in need:
+            v = total[sem] if sem in local else val
+            best[sem] = max(best.get(sem, 0), v)
+        clks = {}
+        for sem, val, clk, _ in need:
+            for s, v in clk.items():
+                if s != sem and s not in local:
+                    clks.setdefault(s, []).append((sem, v))
+        for sem in best:
+            v = best[sem]
+            if known[e].get(sem, 0) >= v:
+                continue
+            if any(o != sem and o in best and x >= v for o, x in clks.get(sem, [])):
+                continue
+            eng[e].wait_ge(T.sem[sem], v)
+        for sem, val, clk, _ in need:
+            for s, v in clk.items():
+                known[e][s] = max(known[e].get(s, 0), v)
+        for sem in best:
+            known[e][sem] = max(known[e].get(sem, 0), best[sem])
+
+    def mark(e, sem, val, r, w):
+        clk = dict(known[e])
+        clk[sem] = val
+        x = (sem, val, clk, e)
+        for t in w:
+            writer[t] = [x]
+            reader[t] = []
+        for t in r:
+            reader.setdefault(t, []).append(x)
+
+    def op(e, call, r, w):
+        gate(e, r, w)
+        s = own_sem[e]
+        total[s] += 1
+        call().then_inc(T.sem[s], 1)
+        mark(e, s, total[s], r, w)
+
+    def dma(e, sem, out, in_, r, w):
+        gate(e, r, w)
+        total[sem] += 16
+        eng[e].dma_start(out, in_).then_inc(T.sem[sem], 16)
+        mark(e, sem, total[sem], r, w)
+
+    def ts(out, in0, s1, o1, r, w, s2=None, o2=None):
+        if o2 is None:
+            op("V", lambda: g.vector.tensor_scalar(out, in0, s1, None, o1), r, w)
+        else:
+            op("V", lambda: g.vector.tensor_scalar(out, in0, s1, s2, o1, o2), r, w)
+
+    def tt(out, in0, in1, o, r, w):
+        op("V", lambda: g.vector.tensor_tensor(out, in0, in1, o), r, w)
+
+    def cp(out, in_, r, w):
+        op("V", lambda: g.vector.tensor_copy(out, in_), r, w)
+
+    def fill(ap, c, w):
+        op("V", lambda: g.vector.memset(ap, c), (), w)
+
+    def act(out, in_, r, w, scale=1.0, bias=0.0):
+        if isinstance(bias, float) and bias == 0.0:
+            op("S", lambda: g.scalar.activation(out, in_, FN.Copy, scale=scale), r, w)
+        else:
+            op("S", lambda: g.scalar.activation(out, in_, FN.Identity, bias=bias, scale=scale), r, w)
+
+    def scan(out, k, d, r, w):
+        op("V", lambda: g.vector.tensor_tensor_scan(out, k, d, 0.0, OP.mult, OP.add), r, w)
+
+    def quant(q, s, a, b, tile, c0, r, w):
+        op("V", lambda: g.vector.quantize_mx(q[:, a:b], s[:, a:b], tile[:, c0:c0 + 4 * (b - a)]), r, w)
+
+    def mm(out, l, ls, la, m, ms, ma, n, r, w, start=True, stop=True):
+        op("T", lambda: g.tensor.matmul_mx(out, l[:, la:la + 128], ls[:, la:la + 128], m[:, ma:ma + n], ms[:, ma:ma + n], start, stop), r, w)
+
+    def evac(e, out, in_, r, w, scale):
+        if e == "S":
+            act(out, in_, r, w, scale=scale)
+        elif scale == 1.0:
+            cp(out, in_, r, w)
+        else:
+            ts(out, in_, scale, OP.mult, r, w)
+
+    ps = [T["ps%d" % b] for b in range(8)]
+
+    dma("Y", "dX", T.win[:, 4 * CEN:4 * (CEN + NC)], T.x[:, :], (), ("xO", "xG"))
+    want = [lambda h: (h // 2 * 2 - 1) % 8, lambda h: h // 2 * 2 + 1, lambda h: (h + 2) % 8 if h % 2 else h,
+            lambda h: h // 2 * 2, lambda h: (h + 1) % 8 if h % 2 else h]
+    n = 0
+    for k in range(5):
+        for h in range(8):
+            f = want[k](h)
+            dma("SY"[n % 2], "dR", T.ri[GRP * h:GRP * h + GRP, 26 * k:26 * k + 26], T.ring[GRP * f:GRP * f + GRP, :], (), (("ri", k, h),))
+            n += 1
+    rit = lambda k: tuple(("ri", k, h) for h in range(8))
+    dma("Y", "dU", T.ut[:, :], T.u[:, :], (), ("ut",))
+    for k, (p0, p1, q0, c, n) in enumerate(shifts(0, NC)):
+        dma("Y", "shG", T.win[p0:p1, c:c + n], T.x[q0:q0 + p1 - p0, :], (), (("shG", k),))
+    NSH = len(shifts(0, NC))
+    dma("Y", "dW", T.wq[:, :].bitcast(dt.uint8), T.wc[:, :], (), ("wq",))
+    dma("Y", "dW", T.wsb[:, :], T.ws[:, :], (), ("wsb",))
+    dma("Y", "dV", T.vt[:, :], T.v[:, :], (), ("vt",))
+
+    fl = dict(allow_small_or_imprecise_dtypes=True)
+    op("G", lambda: g.iota(T.pI[:, :], [[0, 8]], 0, 1), (), ("pI",))
+    op("G", lambda: g.iota(T.idt[:, 0:960], [[1, 960]], 0, 0, **fl), (), ("id0",))
+    op("G", lambda: g.iota(T.jj[:, 0:40], [[1, 5], [1, 8]], 63, 0), (), ("jja",))
+    op("G", lambda: g.iota(T.jj[:, 40:48], [[1, 8]], 64, 0), (), ("jjb",))
+    op("G", lambda: g.iota(T.j20[:, :], [[16, 20]], 0, 1, **fl), (), ("j20",))
+    op("G", lambda: g.iota(T.ji[:, :], [[1, RING]], 512, -1), (), ("ji",))
+    op("G", lambda: g.iota(T.idt[:, 960:2560], [[1, 1600]], 960, 0, **fl), (), ("id1",))
+    fill(T.ew[:, :], 1.0, ("ew",))
+    op("G", lambda: g.affine_select(T.e1[:, :], T.ew[:, :], [[1, 516]], OP.is_equal, 0.0, -3, -4), ("ew",), ("e1",))
+    fill(T.ct[:, 0:512:4], 1.0, (("ct", 0),))
+    fill(T.ct[:, 1:512:4], 1.0, (("ct", 1),))
+    fill(T.ct[0:64, 2:512:4], 0.0, (("ct", 2),))
+    fill(T.ct[64:128, 2:512:4], 1.0, (("ct", 3),))
+    fill(T.ct[:, 3:512:4], 0.0, (("ct", 4),))
+    fill(T.ft[:, :], 0.0, ("ft0", "ft1", "ft2"))
+    fill(T.cst[:, 0:24], -1, ("c0",))
+    fill(T.cst[:, 24:32], 3, ("c1",))
+    fill(T.cst[:, 32:40], 5, ("c2",))
+    fill(T.cst[:, 40:48], 0, ("c3",))
+    fill(T.kp8[:, :], 1.0, ("kp8",))
+    fill(T.kp8[:, 0:48:8], 0.0, ("kp8",))
+    fill(T.keep[:, :], 1.0, ("keep",))
+    fill(T.keep[:, 0:RING:16], 0.0, ("keep",))
+    fill(T.lr[:, :], 0.0, tuple(("lr", k) for k in range(8)) + ("lr",))
+    sc = lambda k: T.sc[:, k:k + 1]
+    ts(T.gI[:, :], T.pI[:, :], 4, OP.arith_shift_right, ("pI",), ("gI",))
+    ts(T.p7[:, :], T.pI[:, :], 7, OP.bitwise_and, ("pI",), ("p7",))
+    ts(T.pr[:, :], T.gI[:, :], 1, OP.bitwise_and, ("gI",), ("pr",))
+    cp(sc(0), T.gI[:, 0:1], ("gI",), ("s0",))
+    ts(T.ul[:, :], T.p7[:, :], 16, OP.mult, ("p7",), ("ul",))
+    cp(sc(1), T.pr[:, 0:1], ("pr",), ("s1",))
+    ts(sc(2), T.gI[:, 0:1], -320.0, OP.mult, ("gI",), ("s2",), float(CEN), OP.add)
+    ts(sc(3), T.pr[:, 0:1], -4800.0, OP.mult, ("pr",), ("s3",), 4800.0, OP.add)
+    ts(sc(4), T.gI[:, 0:1], -16.0, OP.mult, ("gI",), ("s4",), float(CEN), OP.add)
+    ts(sc(5), T.gI[:, 0:1], 0.0, OP.is_equal, ("gI",), ("s5",), 2560.0, OP.mult)
+    tt(sc(6), sc(2), sc(3), OP.add, ("s2", "s3"), ("s6",))
+    ts(sc(7), sc(2), 4.0, OP.mult, ("s2",), ("s7",))
+    tt(sc(8), sc(4), sc(3), OP.add, ("s3", "s4"), ("s8",))
+    ts(sc(9), sc(8), 320.0, OP.add, ("s8",), ("s9",))
+    ts(sc(10), sc(8), -320.0, OP.add, ("s8",), ("s10",))
+    tt(sc(11), sc(10), sc(5), OP.add, ("s5", "s10"), ("s11",))
+    ts(sc(12), sc(4), float(832 - CEN), OP.add, ("s4",), ("s12",))
+    ts(sc(13), T.pr[:, 0:1], -1.0, OP.mult, ("pr",), ("s13",), 1.0, OP.add)
+    act(T.ivA[:, :], T.idt[:, 0:RING], ("id0",), ("ivA",), bias=320.0)
+    act(T.map[:, CEN - NC:CEN + 2 * NC], T.idt[:, 0:960], ("id0",), ("map0",), bias=float(IDB + CEN - NC))
+    act(T.map[:, 0:NC], T.idt[:, 0:NC], ("id0",), ("map1",), bias=float(IDB))
+    act(T.map[:, INV + CEN - NC:INV + CEN + 2 * NC], T.idt[:, 0:960], ("id0",), ("map2",), scale=0.0)
+    act(T.map[:, INV + WINC - NC:INV + WINC], T.idt[:, 0:NC], ("id0",), ("map3",), scale=0.0)
+    act(T.ivB[:, :], T.idt[:, 0:RING], ("id0",), ("ivB",), bias=float(DBL + 320))
+    act(T.ivC[:, :], T.idt[:, 0:RING], ("id0",), ("ivC",), bias=float(2 * DBL + 320))
+    act(T.src[:, IDB + CEN - NC:IDB + CEN + 2 * NC], T.idt[:, 0:960], ("id0",), ("src0",), scale=4.0, bias=float(4 * (CEN - NC)))
+    act(T.src[:, IDB:IDB + NC], T.idt[:, 0:NC], ("id0",), ("src1",), scale=4.0)
+    mapt = ("map0", "map1", "map2", "map3")
+
+    ts(T.xu[:, 0:52], T.ri[:, 0:52], sc(2), OP.add, rit(0) + rit(1) + ("s2",), ("xu0",))
+    ts(T.xu[:, 52:78], T.ri[:, 52:78], sc(6), OP.add, rit(2) + ("s6",), ("xu1",))
+    cp(T.eu[:, :], T.ri[:, 0:78], rit(0) + rit(1) + rit(2), ("eu",))
+    ts(T.xu[:, 78:130], T.ri[:, 78:130], sc(2), OP.add, rit(3) + rit(4) + ("s2",), ("xu2",))
+    for k, nm in enumerate(("ivA", "ivB", "ivC")):
+        op("V", lambda: g.vector.tensor_copy(T.map[:, 0:2 * WINC].indirect(T.xu[:, 26 * k:26 * k + 26]), T[nm][:, :]), (nm, "xu0", "xu1"), mapt)
+        if k == 0:
+            quant(T.qx, T.sx, 0, NC, T.win, 4 * CEN, ("xO", "xG"), ("qxO", "qxG"))
+            quant(T.qu, T.su, 0, 128, T.ut, 0, ("ut",), ("qu",))
+        if k == 1:
+            op("V", lambda: g.vector.tensor_copy(T.qu2[:, 0:128].bitcast(dt.uint32), T.qu[:, 0:128].bitcast(dt.uint32).indirect(T.ul[:, 0:8])), ("qu", "ul"), ("qu2",))
+            op("V", lambda: g.vector.tensor_copy(T.su2[:, 0:128], T.su[:, 0:128].indirect(T.ul[:, 0:8])), ("qu", "ul"), ("su2",))
+    for k in range(3):
+        act(T.src[:, DBL * k:DBL * k + 320], T.idt[:, 0:2560].indirect(T.eu[:, 26 * k + 6:26 * k + 26]), ("id0", "id1", "eu", "s7"), (("sr", k, 0),), scale=4.0, bias=sc(7))
+        act(T.src[:, DBL * k + 320:DBL * k + 736], T.idt[:, 0:2560].indirect(T.eu[:, 26 * k:26 * k + 26]), ("id0", "id1", "eu", "s7"), (("sr", k, 1),), scale=4.0, bias=sc(7))
+    srct = ("src0", "src1") + tuple(("sr", k, i) for k in range(3) for i in range(2))
+    ts(T.ji[:, :], T.ji[:, :], 15, OP.bitwise_and, ("ji",), ("ji",))
+    ts(T.mask[:, :], T.ji[:, :], 0.0, OP.is_equal, ("ji",), ("mask",))
+    ts(T.su3[:, 0:20], T.j20[:, :], sc(8), OP.add, ("j20", "s8"), ("u0",))
+    ts(T.su3[:, 20:40], T.j20[:, :], sc(9), OP.add, ("j20", "s9"), ("u1",))
+    ts(T.su3[:, 40:60], T.j20[:, :], sc(11), OP.add, ("j20", "s11"), ("u2",))
+
+    def look(k, off, n, r, out, w):
+        m, s = T["hm%d" % (k % 2)], T["hs%d" % (k % 2)]
+        tt(m[:, 0:n], T.map[:, 0:2 * WINC].indirect(off), T.mask[:, 0:n], OP.mult, mapt + ("mask",) + r, (("hm", k % 2),))
+        scan(s[:, 0:n], T.keep[:, 0:n], m[:, 0:n], ("keep", ("hm", k % 2)), (("hs", k % 2),))
+        cp(out, s[:, 15:n:16], (("hs", k % 2),), w)
+
+    def counts_a():
+        mm(ps[0][:, 0:128], T.qx, T.sx, 192, T.qu2, T.su2, 0, 128, ("qxO", "qu2", "su2"), (("ps", 0),))
+
+    def counts_b():
+        mm(ps[1][:, 0:128], T.qx, T.sx, 0, T.qu2, T.su2, 0, 128, ("qxG", "qu2", "su2"), (("ps", 1),))
+        mm(ps[2][:, 0:128], T.qx, T.sx, 64, T.qu2, T.su2, 0, 128, ("qxO", "qxG", "qu2", "su2"), (("ps", 2),))
+        for t in range(3):
+            ts(T.ft[:, t:192:4], ps[t][:, 0:48], 0.0, OP.is_gt, (("ps", t),), ("ft%d" % t,))
+        quant(T.qf, T.sf, 0, 128, T.ft, 0, ("ft0", "ft1", "ft2"), ("qf",))
+        mm(ps[3][:, 0:128], T.qc, T.sct, 0, T.qf, T.sf, 0, 128, ("qc", "qf"), (("ps", 3),))
+
+    def counts_c(rd):
+        tt(T.cm[:, :], ps[3][:, 0:48], T.mk[:, :], OP.mult, (("ps", 3), "mk"), ("cm",))
+        scan(T.cs[:, :], T.kp8[:, :], T.cm[:, :], ("cm", "kp8"), ("cs",))
+
+    quant(T.qc, T.sct, 0, 128, T.ct, 0, tuple(("ct", k) for k in range(5)), ("qc",))
+    counts_a()
+    counts_b()
+    ts(T.cst[:, :], T.cst[:, :], sc(1), OP.mult, ("c0", "c1", "c2", "c3", "s1"), ("c0",))
+    tt(T.jj[:, :], T.jj[:, :], T.cst[:, :], OP.subtract, ("jja", "jjb", "c0"), ("jja",))
+    ts(T.jj[:, :], T.jj[:, :], sc(0), OP.subtract, ("jja", "s0"), ("jja",))
+    ts(T.jj[:, :], T.jj[:, :], 7, OP.bitwise_and, ("jja",), ("jja",))
+    ts(T.mk[:, :], T.jj[:, :], 0.0, OP.is_equal, ("jja",), ("mk",))
+
+    look(0, T.su3[:, 20:40], NC, ("u1",), T.pm[:, 0:20], ("pm0",))
+    look(1, T.su3[:, 40:60], NC, ("u2",), T.pm[:, 20:40], ("pm1",))
+    for k, h in enumerate((1, 3, 5, 7)):
+        f = (h + 1) % 8
+        dma("Y", "dL", T.lr[GRP * h:GRP * h + GRP, 0:20], T.pm[GRP * (h - 1):GRP * h, 0:20], ("pm0", "lr"), (("lr", k),))
+        dma("Y", "dL", T.lr[GRP * h:GRP * h + GRP, 20:40], T.pm[GRP * f:GRP * f + GRP, 20:40], ("pm1", "lr"), (("lr", 4 + k),))
+    look(0, T.xu[:, 78:104], RING, ("xu2",), T.bA[:, 0:26], ("bA0",))
+    look(1, T.xu[:, 104:130], RING, ("xu2",), T.bA[:, 26:52], ("bA1",))
+    look(0, T.su3[:, 0:20], NC, ("u0",), T.bA[:, 52:72], ("bA2",))
+    bAt = ("bA0", "bA1", "bA2")
+    ts(T.mA[:, 0:26], T.bA[:, 0:26], float(DBL), OP.is_lt, bAt, ("mA",))
+    ts(T.g1[:, :], T.bA[:, :], float(DBL), OP.is_ge, bAt, ("g1",))
+    ts(T.g2[:, :], T.bA[:, :], float(2 * DBL), OP.is_ge, bAt, ("g2",))
+    ts(T.g3[:, :], T.bA[:, :], float(3 * DBL), OP.is_ge, bAt, ("g3",))
+    tt(T.mB[:, :], T.g1[:, :], T.g2[:, :], OP.subtract, ("g1", "g2"), ("mB",))
+    tt(T.mC[:, :], T.g2[:, :], T.g3[:, :], OP.subtract, ("g2", "g3"), ("mC",))
+
+    def even_lists():
+        b = lambda k: T.bt[:, 20 * k:20 * k + 20]
+        lrt = tuple(("lr", k) for k in range(8)) + ("lr",)
+        ts(b(0), T.bA[:, 52:72], sc(13), OP.mult, ("bA2", "s13"), ("b0",))
+        ts(T.j832[:, :], T.j20[:, :], sc(12), OP.add, ("j20", "s12"), ("j832",))
+        tt(b(1), b(0), T.lr[:, 0:20], OP.add, ("b0",) + lrt, ("b1",))
+        ts(T.mE[:, :], T.lr[:, 20:40], 0.0, OP.is_gt, lrt, ("mE",))
+        ts(b(3), T.lr[:, 20:40], float(2 * DBL + 320 - RING), OP.subtract, lrt, ("b3",), 0.0, OP.max)
+        ts(T.mD[:, :], b(1), 0.0, OP.is_gt, ("b1",), ("mD",))
+        ts(b(2), b(1), float(2 * DBL + 320), OP.subtract, ("b1",), ("b2",), 0.0, OP.max)
+        tt(b(4), T.mD[:, :], T.mE[:, :], OP.add, ("mD", "mE"), ("b4",))
+        tt(b(7), b(2), b(3), OP.add, ("b2", "b3"), ("b7",))
+        ts(b(5), b(4), -1.0, OP.mult, ("b4",), ("b5",), 1.0, OP.add)
+        ts(b(9), T.mE[:, :], float(RING), OP.mult, ("mE",), ("b9",))
+        tt(b(6), b(5), T.j832[:, :], OP.mult, ("b5", "j832"), ("b6",))
+        ts(b(8), b(5), -100000.0, OP.mult, ("b5",), ("b8",))
+        tt(T.bB[:, :], b(6), b(7), OP.add, ("b6", "b7"), ("bB",))
+        tt(T.thr[:, :], b(8), b(9), OP.add, ("b8", "b9"), ("thr",))
+
+    cs = lambda k: T.cs[:, 8 * k + 7:8 * k + 8]
+    SPL = 44
+
+    def lists_a():
+        ts(T.ta[:, :], T.mB[:, :], cs(0), OP.mult, ("mB", "cs"), ("ta",))
+        ts(T.tb[:, 0:26], T.mA[:, 0:26], cs(2), OP.mult, ("mA", "cs"), ("tb0",))
+        ts(T.tb[:, 26:52], T.mC[:, 26:52], cs(4), OP.mult, ("mC", "cs"), ("tb1",))
+        tt(T.tc[:, :], T.bA[:, :], T.ta[:, :], OP.subtract, bAt + ("ta",), ("tc",))
+        tt(T.tc[:, 0:52], T.tc[:, 0:52], T.tb[:, 0:52], OP.subtract, ("tc", "tb0", "tb1"), ("tc",))
+        cp(T.oA[:, :], T.tc[:, :], ("tc",), ("oA",))
+        act(T.tab[:, 0:16 * SPL], T.src[:, :].indirect(T.oA[:, 0:SPL]), srct + ("oA",), ("tab0",))
+
+    def lists_b():
+        ts(T.td[:, :], T.mD[:, :], cs(1), OP.mult, ("mD", "cs"), ("td",))
+        ts(T.te[:, :], T.mE[:, :], cs(3), OP.mult, ("mE", "cs"), ("te",))
+        tt(T.tt[:, :], T.bB[:, :], T.td[:, :], OP.subtract, ("bB", "td"), ("tt",))
+        tt(T.tt[:, :], T.tt[:, :], T.te[:, :], OP.subtract, ("tt", "te"), ("tt",))
+        tt(T.tw[:, :], T.tt[:, :], T.thr[:, :], OP.is_lt, ("tt", "thr"), ("tw",))
+        ts(T.tw[:, :], T.tw[:, :], float(RING), OP.mult, ("tw",), ("tw",))
+        tt(T.tt[:, :], T.tt[:, :], T.tw[:, :], OP.add, ("tt", "tw"), ("tt",))
+        cp(T.oB[:, :], T.tt[:, :], ("tt",), ("oB",))
+
+    def lists_c():
+        cp(T.tab[:, 16 * SPL:1152], T.src[:, :].indirect(T.oA[:, SPL:72]), srct + ("oA",), ("tab1",))
+
+    def turn(h, tile, tok):
+        m, s = T.bm[:, HALF * h:HALF * h + HALF], T.bs
+        tt(m, T.tab[:, :].indirect(T.oB[:, 10 * h:10 * h + 10]), T.mask[:, 0:HALF], OP.mult, ("tab0", "tab1", "oB", "mask"), (("bm", h),))
+        scan(s[:, HALF * h:HALF * h + HALF], T.keep[:, 0:HALF], m, ("keep", ("bm", h)), (("bs", h),))
+        for t in (2, 0, 3, 1):
+            c = 40 * h + 10 * t
+            ts(T.l4[:, c:c + 10], s[:, HALF * h + 15:HALF * h + HALF:16], float(t), OP.add, (("bs", h),), (("l4", h, t),))
+        wt = ("xO", "xG") + tuple((n, k) for n in ("shO", "shG") for k in range(NSH))
+        for t in (2, 0, 3, 1):
+            c = 40 * h + 10 * t
+            src = T.win[:, :].indirect(T.l4[:, c:c + 10])
+            if t >= 2:
+                act(tile[:, t:4 * HALF:4], src, wt + (("l4", h, t),), ((tok, t),))
+            else:
+                cp(tile[:, t:4 * HALF:4], src, wt + (("l4", h, t),), ((tok, t),))
+
+    def unpack(q, s, qt, base, tile, tok):
+        for b in range(4):
+            mm(ps[base + b][:, 0:HALF], T.qe, T.se, 128 * b, q, s, 0, HALF, (("qe", b),) + qt, (("ps", base + b),))
+        for b in range(4):
+            evac("VS"[b % 2], tile[:, b:4 * HALF:4], ps[base + b][:, 0:HALF], (("ps", base + b),), ((tok, b),), 1.0)
+
+    def first(base, q, s, qt):
+        for b in range(4):
+            mm(ps[base + b][:, 0:HALF], T.qe, T.se, 512 + 128 * b, q, s, 0, HALF, (("qe", 4 + b),) + qt, (("ps", base + b),), True, False)
+
+    def layer(base, q, s, qt, c0, tok):
+        for b in range(4):
+            mm(ps[base + b][:, 0:HALF], T.wq, T.wsb, 128 * b, q, s, 0, HALF, ("wq", "wsb") + qt, (("ps", base + b),), False, True)
+        for b in range(4):
+            evac("VS"[b % 2], T.win[:, c0 + b:c0 + 4 * HALF:4], ps[base + b][:, 0:HALF], (("ps", base + b),), ((tok, b),), 2.0 ** -5)
+
+    four = lambda t: tuple((t, b) for b in range(4))
+
+    for rd in range(3):
+        last = rd == 2
+        counts_c(rd)
+        if rd == 0:
+            lists_a()
+            even_lists()
+        else:
+            lists_a()
+        lists_b()
+        lists_c()
+        turn(0, T.gr, "gr")
+        if rd == 0:
+            act(T.e32[:, :], T.e1[:, :], ("e1",), ("e32",), scale=32.0)
+            for b in range(4):
+                quant(T.qe, T.se, 128 * b, 128 * b + 128, T.e1, 3 - b, ("e1",), (("qe", b),))
+        quant(T.q1, T.s1, 0, HALF, T.gr, 0, four("gr"), ("q1",))
+        unpack(T.q1, T.s1, ("q1",), 4, T.gt, "gt")
+        quant(T.q2, T.s2, 0, HALF, T.gt, 0, four("gt"), ("q2",))
+        dst = T.cores[rank ^ MASKS[rd]]
+        rid, pid = topo.addr(dst)[0], topo.addr(dst)[1]
+        ne, mask = len(topo.engines(core, dst)), topo.mask(core, dst)
+        arr = "arr%d" % rd
+        gate("G", ("q2",), ())
+        g.remote_dma(T["lc%d" % rd][:, :].bitcast(dt.uint8), T.q2[:, :].bitcast(dt.uint8), T.sem[arr], T.sem.sent, pid, rid, mask)
+        g.remote_dma(T["ls%d" % rd][:, :], T.s2[:, :], T.sem[arr], T.sem.sent, pid, rid, mask)
+        total["sent"] += 2 * ne
+        total[arr] += 2 * ne
+        mark("G", "sent", total["sent"], ("q2",), ())
+        land = ("land", rd)
+        writer[land] = [(arr, 2 * ne, {}, "R")]
+        if rd == 0:
+            for b in range(4):
+                quant(T.qe, T.se, 512 + 128 * b, 640 + 128 * b, T.e32, 3 - b, ("e32",), (("qe", 4 + b),))
+        turn(1, T.ow, "ow")
+        quant(T.qo, T.so, 0, HALF, T.ow, 0, four("ow"), ("qo",))
+        unpack(T.qo, T.so, ("qo",), 0, T.zo, "zo")
+        first(0, T.qo, T.so, ("qo",))
+        quant(T.qzo, T.szo, 0, HALF, T.zo, 0, four("zo"), ("qzo",))
+        layer(0, T.qzo, T.szo, ("qzo",), 4 * (CEN + HALF), "xo")
+        for t in ("xO",):
+            writer[t], reader[t] = sum([writer[("xo", b)] for b in range(4)], []), []
+        if not last:
+            for k, (p0, p1, q0, c, n) in enumerate(shifts(HALF, NC)):
+                dma("Y", "shO", T.win[p0:p1, c:c + n], T.win[q0:q0 + p1 - p0, 4 * (CEN + HALF):4 * (CEN + NC)], ("xO",), (("shO", k),))
+        quant(T.qx, T.sx, HALF, NC, T.win, 4 * (CEN + HALF), ("xO",), ("qxO",))
+        act(T.acs[:, rd:rd + 1], cs(5), ("cs",), (("ac", rd),))
+        if rd == 0:
+            quant(T.qv, T.sv, 0, 128, T.vt, 0, ("vt",), ("qv",))
+        if last:
+            dma("Y", "dOut", T.oc[:, 4 * HALF:4 * NC], T.qx[:, HALF:NC].bitcast(dt.uint8), ("qxO",), ("oco",))
+            for k in range(4):
+                dma("Y", "dOut", T.osc[4 * k:4 * k + 4, HALF:NC], T.sx[32 * k:32 * k + 4, HALF:NC], ("qxO",), (("oso", k),))
+            dma("Y", "dOut", T.ac[:, :], T.acs[0:128:16, 0:3], (("ac", 0), ("ac", 1), ("ac", 2)), ("aco",))
+            mm(ps[0][:, 0:HALF], T.qv, T.sv, 0, T.qx, T.sx, HALF, HALF, ("qv", "qxO"), (("ps", 0),))
+            act(T.yt[:, HALF:NC], ps[0][:, 0:HALF], (("ps", 0),), ("yO",))
+            dma("Y", "dOut", T.y[:, HALF:NC], T.yt[:, HALF:NC], ("yO",), ("you",))
+        else:
+            counts_a()
+        unpack(T["lc%d" % rd], T["ls%d" % rd], (land,), 4, T.zg, "zg")
+        first(4, T["lc%d" % rd], T["ls%d" % rd], (land,))
+        quant(T.qzg, T.szg, 0, HALF, T.zg, 0, four("zg"), ("qzg",))
+        layer(4, T.qzg, T.szg, ("qzg",), 4 * CEN, "xg")
+        for t in ("xG",):
+            writer[t], reader[t] = sum([writer[("xg", b)] for b in range(4)], []), []
+        if not last:
+            for k, (p0, p1, q0, c, n) in enumerate(shifts(0, HALF)):
+                dma("Y", "shG", T.win[p0:p1, c:c + n], T.win[q0:q0 + p1 - p0, 4 * CEN:4 * (CEN + HALF)], ("xG",), (("shG", k),))
+        quant(T.qx, T.sx, 0, HALF, T.win, 4 * CEN, ("xG",), ("qxG",))
+        if last:
+            dma("Y", "dOut", T.oc[:, 0:4 * HALF], T.qx[:, 0:HALF].bitcast(dt.uint8), ("qxG",), ("ocg",))
+            for k in range(4):
+                dma("S", "dOut", T.osc[4 * k:4 * k + 4, 0:HALF], T.sx[32 * k:32 * k + 4, 0:HALF], ("qxG",), (("osg", k),))
+            mm(ps[1][:, 0:HALF], T.qv, T.sv, 0, T.qx, T.sx, 0, HALF, ("qv", "qxG"), (("ps", 1),))
+            cp(T.yt[:, 0:HALF], ps[1][:, 0:HALF], (("ps", 1),), ("yG",))
+            dma("Y", "dOut", T.y[:, 0:HALF], T.yt[:, 0:HALF], ("yG",), ("yog",))
+        else:
+            counts_b()
+    for s in SEMAPHORES:
+        if total[s] and known["Y"].get(s, 0) < total[s]:
+            g.sync.wait_ge(T.sem[s], total[s])

@@ -139,7 +139,8 @@ def rank_program(g, core, T, topo):
         mark(e, s, total[s], r, w)
 
     def dma(e, sem, out, in_, r, w):
-        gate(e, r, w)
+        if sem not in ("shO", "shG"):
+            gate(e, r, w)
         total[sem] += 16
         eng[e].dma_start(out, in_).then_inc(T.sem[sem], 16)
         mark(e, sem, total[sem], r, w)
@@ -446,6 +447,7 @@ def rank_program(g, core, T, topo):
         for t in ("xO",):
             writer[t], reader[t] = sum([writer[("xo", b)] for b in range(4)], []), []
         if not last:
+            gate("Y", ("xO",), tuple(("shO", k) for k in range(NSH)))
             for k, (p0, p1, q0, c, n) in enumerate(shifts(HALF, NC)):
                 dma("Y", "shO", T.win[p0:p1, c:c + n], T.win[q0:q0 + p1 - p0, 4 * (CEN + HALF):4 * (CEN + NC)], ("xO",), (("shO", k),))
         quant(T.qx, T.sx, HALF, NC, T.win, 4 * (CEN + HALF), ("xO",), ("qxO",))
@@ -469,6 +471,7 @@ def rank_program(g, core, T, topo):
         for t in ("xG",):
             writer[t], reader[t] = sum([writer[("xg", b)] for b in range(4)], []), []
         if not last:
+            gate("Y", ("xG",), tuple(("shG", k) for k in range(NSH)))
             for k, (p0, p1, q0, c, n) in enumerate(shifts(0, HALF)):
                 dma("Y", "shG", T.win[p0:p1, c:c + n], T.win[q0:q0 + p1 - p0, 4 * CEN:4 * (CEN + HALF)], ("xG",), (("shG", k),))
         quant(T.qx, T.sx, 0, HALF, T.win, 4 * CEN, ("xG",), ("qxG",))

@@ -8,6 +8,7 @@ CEN = 7 * NC
 WINC = 15 * NC
 IDB = 3 * DBL
 INV = WINC
+ABS = 2500
 OP = AluOpType
 FN = ActivationFunctionType
 
@@ -16,24 +17,22 @@ SCRATCH = {
     "map": ("sbuf", [128, 2 * WINC], "float32"),
     "src": ("sbuf", [128, IDB + WINC], "float32"),
     "idt": ("sbuf", [128, 2560], "float32"),
-    "ivA": ("sbuf", [128, RING], "float32"), "ivB": ("sbuf", [128, RING], "float32"), "ivC": ("sbuf", [128, RING], "float32"),
-    "ri": ("sbuf", [128, 130], "int32"), "eu": ("sbuf", [128, 78], "uint16"), "xu": ("sbuf", [128, 130], "uint16"),
-    "su3": ("sbuf", [128, 60], "uint16"),
+    "iv1": ("sbuf", [128, RING], "float32"), "iv2": ("sbuf", [128, RING], "float32"),
+    "ri": ("sbuf", [128, 130], "int32"), "eu": ("sbuf", [128, 78], "uint16"), "xu": ("sbuf", [128, 52], "uint16"),
+    "kl": ("sbuf", [128, 40], "int32"), "xk": ("sbuf", [128, 40], "uint16"), "xe": ("sbuf", [128, 40], "uint16"),
     "pI": ("sbuf", [128, 8], "int32"), "gI": ("sbuf", [128, 8], "int32"), "pr": ("sbuf", [128, 8], "int32"), "p7": ("sbuf", [128, 8], "int32"),
-    "ul": ("sbuf", [128, 8], "uint16"),
+    "kI": ("sbuf", [128, 8], "int32"), "ul": ("sbuf", [128, 8], "uint16"),
     "sc": ("sbuf", [128, 32], "float32"),
     "jj": ("sbuf", [128, 48], "int32"), "cst": ("sbuf", [128, 48], "int32"), "mk": ("sbuf", [128, 48], "float32"), "kp8": ("sbuf", [128, 48], "float32"),
-    "ji": ("sbuf", [128, RING], "int32"), "mask": ("sbuf", [128, RING], "float32"), "keep": ("sbuf", [128, RING], "float32"),
+    "jm": ("sbuf", [128, 640], "float32"), "jd": ("sbuf", [128, 640], "float32"), "mask": ("sbuf", [128, 640], "float32"), "keep": ("sbuf", [128, 640], "float32"),
     "j20": ("sbuf", [128, 20], "float32"), "j832": ("sbuf", [128, 20], "float32"),
-    "hm0": ("sbuf", [128, RING], "float32"), "hs0": ("sbuf", [128, RING], "float32"),
-    "hm1": ("sbuf", [128, RING], "float32"), "hs1": ("sbuf", [128, RING], "float32"),
-    "bA": ("sbuf", [128, 72], "float32"), "mA": ("sbuf", [128, 72], "float32"), "mB": ("sbuf", [128, 72], "float32"),
-    "g1": ("sbuf", [128, 72], "float32"), "g2": ("sbuf", [128, 72], "float32"), "g3": ("sbuf", [128, 72], "float32"), "mC": ("sbuf", [128, 72], "float32"),
-    "pm": ("sbuf", [128, 40], "float32"), "lr": ("sbuf", [128, 40], "float32"),
-    "bt": ("sbuf", [128, 240], "float32"),
-    "bB": ("sbuf", [128, 20], "float32"), "mD": ("sbuf", [128, 20], "float32"), "mE": ("sbuf", [128, 20], "float32"), "thr": ("sbuf", [128, 20], "float32"),
-    "ta": ("sbuf", [128, 72], "float32"), "tb": ("sbuf", [128, 72], "float32"), "tc": ("sbuf", [128, 72], "float32"),
-    "td": ("sbuf", [128, 20], "float32"), "te": ("sbuf", [128, 20], "float32"), "tt": ("sbuf", [128, 20], "float32"), "tw": ("sbuf", [128, 20], "float32"),
+    "hm0": ("sbuf", [128, 640], "float32"), "hs0": ("sbuf", [128, 640], "float32"),
+    "hm1": ("sbuf", [128, 640], "float32"), "hs1": ("sbuf", [128, 640], "float32"),
+    "ph": ("sbuf", [128, 52], "float32"), "pe": ("sbuf", [128, 40], "float32"), "lt": ("sbuf", [128, 20], "float32"), "rt": ("sbuf", [128, 20], "float32"),
+    "w1": ("sbuf", [128, 26], "float32"), "w2": ("sbuf", [128, 26], "float32"), "w3": ("sbuf", [128, 26], "float32"), "w4": ("sbuf", [128, 26], "float32"),
+    "bA": ("sbuf", [128, 92], "float32"), "mL": ("sbuf", [128, 92], "float32"), "mR": ("sbuf", [128, 92], "float32"),
+    "g1": ("sbuf", [128, 72], "float32"), "g2": ("sbuf", [128, 72], "float32"), "g3": ("sbuf", [128, 72], "float32"),
+    "ta": ("sbuf", [128, 92], "float32"), "tb": ("sbuf", [128, 92], "float32"), "tq": ("sbuf", [128, 92], "float32"), "tw": ("sbuf", [128, 20], "float32"), "te": ("sbuf", [128, 20], "float32"),
     "oA": ("sbuf", [128, 72], "uint16"), "oB": ("sbuf", [128, 20], "uint16"), "l4": ("sbuf", [128, 80], "uint16"),
     "tab": ("sbuf", [128, 1152], "float32"),
     "bm": ("sbuf", [128, 2 * HALF], "float32"), "bs": ("sbuf", [128, 2 * HALF], "float32"),
@@ -60,7 +59,7 @@ for _r in range(3):
     SCRATCH["ls%d" % _r] = ("sbuf", [128, HALF], "uint8")
 for _b in range(8):
     SCRATCH["ps%d" % _b] = ("psum", [128, 512], "float32")
-SEMAPHORES = ["cV", "cS", "cT", "cG", "dX", "dR", "dU", "dV", "dW", "shO", "shG", "dL", "dOut", "arr0", "arr1", "arr2", "sent"]
+SEMAPHORES = ["cV", "cS", "cT", "cG", "dX", "dR", "dQ", "dH", "dU", "dV", "dW", "shO", "shG", "dL", "dE", "dOut", "arr0", "arr1", "arr2", "sent"]
 
 
 def shifts(lo, hi):
@@ -88,7 +87,7 @@ def rank_program(g, core, T, topo):
     eng = {"V": g.vector, "S": g.scalar, "T": g.tensor, "G": g, "Y": g.sync}
     own_sem = {"V": "cV", "S": "cS", "T": "cT", "G": "cG"}
     total = {s: 0 for s in SEMAPHORES}
-    local = ("dX", "dR", "dU", "dV", "dW", "shO", "shG", "dL", "dOut")
+    local = ("dX", "dR", "dQ", "dH", "dU", "dV", "dW", "shO", "shG", "dL", "dE", "dOut")
     known = {e: {} for e in eng}
     writer, reader = {}, {}
 
@@ -160,11 +159,11 @@ def rank_program(g, core, T, topo):
     def fill(ap, c, w):
         op("V", lambda: g.vector.memset(ap, c), (), w)
 
-    def act(out, in_, r, w, scale=1.0, bias=0.0):
-        if isinstance(bias, float) and bias == 0.0:
-            op("S", lambda: g.scalar.activation(out, in_, FN.Copy, scale=scale), r, w)
+    def act(out, in_, r, w, scale=1.0, bias=None, fn=None):
+        if bias is None:
+            op("S", lambda: g.scalar.activation(out, in_, fn or FN.Copy, scale=scale), r, w)
         else:
-            op("S", lambda: g.scalar.activation(out, in_, FN.Identity, bias=bias, scale=scale), r, w)
+            op("S", lambda: g.scalar.activation(out, in_, fn or FN.Identity, bias=bias, scale=scale), r, w)
 
     def scan(out, k, d, r, w):
         op("V", lambda: g.vector.tensor_tensor_scan(out, k, d, 0.0, OP.mult, OP.add), r, w)
@@ -184,33 +183,84 @@ def rank_program(g, core, T, topo):
             ts(out, in_, scale, OP.mult, r, w)
 
     ps = [T["ps%d" % b] for b in range(8)]
-
-    dma("Y", "dX", T.win[:, 4 * CEN:4 * (CEN + NC)], T.x[:, :], (), ("xO", "xG"))
-    want = [lambda h: (h // 2 * 2 - 1) % 8, lambda h: h // 2 * 2 + 1, lambda h: (h + 2) % 8 if h % 2 else h,
-            lambda h: h // 2 * 2, lambda h: (h + 1) % 8 if h % 2 else h]
-    n = 0
-    for k in range(5):
-        for h in range(8):
-            f = want[k](h)
-            dma("SY"[n % 2], "dR", T.ri[GRP * h:GRP * h + GRP, 26 * k:26 * k + 26], T.ring[GRP * f:GRP * f + GRP, :], (), (("ri", k, h),))
-            n += 1
-    rit = lambda k: tuple(("ri", k, h) for h in range(8))
-    dma("Y", "dU", T.ut[:, :], T.u[:, :], (), ("ut",))
-    for k, (p0, p1, q0, c, n) in enumerate(shifts(0, NC)):
-        dma("Y", "shG", T.win[p0:p1, c:c + n], T.x[q0:q0 + p1 - p0, :], (), (("shG", k),))
+    sc = lambda k: T.sc[:, k:k + 1]
     NSH = len(shifts(0, NC))
-    dma("Y", "dW", T.wq[:, :].bitcast(dt.uint8), T.wc[:, :], (), ("wq",))
-    dma("Y", "dW", T.wsb[:, :], T.ws[:, :], (), ("wsb",))
-    dma("Y", "dV", T.vt[:, :], T.v[:, :], (), ("vt",))
+
+    def ring(q, sem, k, p0, p1, q0, tok):
+        dma(q, sem, T.ri[p0:p1, 26 * k:26 * k + 26], T.ring[q0:q0 + p1 - p0, :], (), (tok,))
+    for f in (1, 3, 5, 7):
+        ring("S", "dR", 3, GRP * f, GRP * f + GRP, GRP * f, ("l1", f))
+        e = (f + 1) % 8
+        ring("Y", "dR", 3, GRP * e, GRP * e + GRP, GRP * f, ("l1", e))
+    ring("S", "dR", 4, 0, 128 - GRP, GRP, "l2a")
+    ring("Y", "dR", 4, 128 - GRP, 128, 0, "l2b")
+    dma("Y", "dX", T.win[:, 4 * CEN:4 * (CEN + NC)], T.x[:, :], (), ("xO", "xG"))
+    dma("Y", "dU", T.ut[:, :], T.u[:, :], (), ("ut",))
+    n = 0
+    for k, src in ((0, -1), (1, 1)):
+        for h in range(8):
+            f = (h // 2 * 2 + src) % 8
+            ring("SY"[n % 2], "dQ", k, GRP * h, GRP * h + GRP, GRP * f, ("q", k, h))
+            n += 1
+    ring("S", "dQ", 2, 0, 128 - 2 * GRP, 2 * GRP, "l3a")
+    ring("Y", "dQ", 2, 128 - 2 * GRP, 128, 0, "l3b")
+    qtok = tuple(("q", k, h) for k in range(2) for h in range(8)) + ("l3a", "l3b")
 
     fl = dict(allow_small_or_imprecise_dtypes=True)
     op("G", lambda: g.iota(T.pI[:, :], [[0, 8]], 0, 1), (), ("pI",))
-    op("G", lambda: g.iota(T.idt[:, 0:960], [[1, 960]], 0, 0, **fl), (), ("id0",))
+    op("G", lambda: g.iota(T.idt[:, 0:RING], [[1, RING]], 0, 0, **fl), (), ("id0",))
+    op("G", lambda: g.iota(T.j20[:, :], [[16, 20]], 0, 1, **fl), (), ("j20",))
+    op("G", lambda: g.iota(T.jm[:, :], [[0, 40], [1, 16]], 0, 0, **fl), (), ("jm",))
     op("G", lambda: g.iota(T.jj[:, 0:40], [[1, 5], [1, 8]], 63, 0), (), ("jja",))
     op("G", lambda: g.iota(T.jj[:, 40:48], [[1, 8]], 64, 0), (), ("jjb",))
-    op("G", lambda: g.iota(T.j20[:, :], [[16, 20]], 0, 1, **fl), (), ("j20",))
-    op("G", lambda: g.iota(T.ji[:, :], [[1, RING]], 512, -1), (), ("ji",))
-    op("G", lambda: g.iota(T.idt[:, 960:2560], [[1, 1600]], 960, 0, **fl), (), ("id1",))
+    op("G", lambda: g.iota(T.idt[:, RING:2560], [[1, 2560 - RING]], RING, 0, **fl), (), ("id1",))
+    ts(T.gI[:, :], T.pI[:, :], 4, OP.arith_shift_right, ("pI",), ("gI",))
+    ts(T.kI[:, :], T.pI[:, :], 15, OP.bitwise_and, ("pI",), ("kI",))
+    ts(T.p7[:, :], T.pI[:, :], 7, OP.bitwise_and, ("pI",), ("p7",))
+    ts(T.pr[:, :], T.gI[:, :], 1, OP.bitwise_and, ("gI",), ("pr",))
+    gc, pc = T.gI[:, 0:1], T.pr[:, 0:1]
+    ts(sc(2), gc, -320.0, OP.mult, ("gI",), ("s2",), float(CEN), OP.add)
+    ts(sc(15), gc, 304.0, OP.mult, ("gI",), ("s15",))
+    ts(sc(19), T.kI[:, 0:1], -1.0, OP.mult, ("kI",), ("s19",))
+    ts(sc(20), pc, float(DBL), OP.mult, ("pr",), ("s20",), 320.0, OP.add)
+    ts(sc(21), pc, -float(DBL + 320), OP.mult, ("pr",), ("s21",), float(DBL + 320), OP.add)
+    ts(sc(24), pc, float(INV), OP.mult, ("pr",), ("s24",))
+    ts(T.kl[:, 0:20], T.j20[:, :], sc(15), OP.add, ("j20", "s15"), ("kl0",))
+    tt(sc(14), sc(2), sc(24), OP.add, ("s2", "s24"), ("s14",))
+    tt(sc(16), sc(15), sc(24), OP.add, ("s15", "s24"), ("s16",))
+    ts(sc(7), sc(2), 4.0, OP.mult, ("s2",), ("s7",))
+    ts(T.kl[:, 20:40], T.j20[:, :], sc(16), OP.add, ("j20", "s16"), ("kl1",))
+    cp(sc(0), gc, ("gI",), ("s0",))
+    cp(sc(1), pc, ("pr",), ("s1",))
+    ts(sc(4), gc, -16.0, OP.mult, ("gI",), ("s4",), float(CEN), OP.add)
+    ts(sc(5), gc, 7.0, OP.is_equal, ("gI",), ("s5",), -2560.0, OP.mult)
+    ts(sc(6), pc, float(INV + NC), OP.mult, ("pr",), ("s6",))
+    ts(sc(8), pc, 320.0, OP.mult, ("pr",), ("s8",))
+    tt(sc(9), sc(4), sc(5), OP.add, ("s4", "s5"), ("s9",))
+    ts(sc(12), gc, -16.0, OP.mult, ("gI",), ("s12",), 832.0, OP.add)
+    ts(sc(22), gc, 0.0, OP.is_equal, ("gI",), ("s22",), -2560.0, OP.mult)
+    tt(sc(17), sc(9), sc(6), OP.add, ("s9", "s6"), ("s17",))
+    ts(sc(23), pc, -10000.0, OP.mult, ("pr",), ("s23",), 10001.0, OP.add)
+    ts(sc(25), sc(22), -416.0, OP.add, ("s22",), ("s25",))
+    tt(sc(18), sc(17), sc(8), OP.add, ("s17", "s8"), ("s18",))
+    ts(T.ul[:, :], T.p7[:, :], 16, OP.mult, ("p7",), ("ul",))
+    for h in (0, 2, 4, 6):
+        dma("Y", "dH", T.kl[GRP * h:GRP * h + GRP, 0:26], T.ring[GRP * h:GRP * h + GRP, :], ("kl0", "kl1"), (("kh", h),))
+    klt = ("kl0", "kl1") + tuple(("kh", h) for h in (0, 2, 4, 6))
+    for k, (p0, p1, q0, c, n) in enumerate(shifts(0, NC)):
+        dma("Y", "shG", T.win[p0:p1, c:c + n], T.x[q0:q0 + p1 - p0, :], (), (("shG", k),))
+    dma("Y", "dW", T.wq[:, :].bitcast(dt.uint8), T.wc[:, :], (), ("wq",))
+    dma("Y", "dW", T.wsb[:, :], T.ws[:, :], (), ("wsb",))
+    dma("Y", "dV", T.vt[:, :], T.v[:, :], (), ("vt",))
+    act(T.iv1[:, :], T.idt[:, 0:RING], ("id0", "s20"), ("iv1",), bias=sc(20))
+    act(T.map[:, CEN:CEN + NC], T.idt[:, 0:NC], ("id0",), ("map0",), bias=float(IDB + CEN))
+    for k, c in enumerate((INV + CEN, INV + CEN + 2 * NC, INV + NC)):
+        act(T.map[:, c:c + NC], T.idt[:, 0:NC], ("id0",), ("map%d" % (k + 1),), scale=0.0, bias=float(ABS))
+    act(T.iv2[:, :], T.idt[:, 0:RING], ("id0", "s21"), ("iv2",), bias=sc(21))
+    act(T.jd[:, :], T.jm[:, :], ("jm", "s19"), ("jd",), bias=sc(19), fn=FN.Abs)
+    act(T.mask[:, :], T.jd[:, :], ("jd",), ("mask",), scale=-1.0, bias=1.0, fn=FN.Relu)
+    act(T.keep[:, :], T.jm[:, :], ("jm",), ("keep",), fn=FN.Sign)
+    mapt = tuple("map%d" % k for k in range(4))
     fill(T.ew[:, :], 1.0, ("ew",))
     op("G", lambda: g.affine_select(T.e1[:, :], T.ew[:, :], [[1, 516]], OP.is_equal, 0.0, -3, -4), ("ew",), ("e1",))
     fill(T.ct[:, 0:512:4], 1.0, (("ct", 0),))
@@ -218,73 +268,42 @@ def rank_program(g, core, T, topo):
     fill(T.ct[0:64, 2:512:4], 0.0, (("ct", 2),))
     fill(T.ct[64:128, 2:512:4], 1.0, (("ct", 3),))
     fill(T.ct[:, 3:512:4], 0.0, (("ct", 4),))
-    fill(T.ft[:, :], 0.0, ("ft0", "ft1", "ft2"))
     fill(T.cst[:, 0:24], -1, ("c0",))
     fill(T.cst[:, 24:32], 3, ("c1",))
     fill(T.cst[:, 32:40], 5, ("c2",))
     fill(T.cst[:, 40:48], 0, ("c3",))
-    fill(T.kp8[:, :], 1.0, ("kp8",))
-    fill(T.kp8[:, 0:48:8], 0.0, ("kp8",))
-    fill(T.keep[:, :], 1.0, ("keep",))
-    fill(T.keep[:, 0:RING:16], 0.0, ("keep",))
-    fill(T.lr[:, :], 0.0, tuple(("lr", k) for k in range(8)) + ("lr",))
-    sc = lambda k: T.sc[:, k:k + 1]
-    ts(T.gI[:, :], T.pI[:, :], 4, OP.arith_shift_right, ("pI",), ("gI",))
-    ts(T.p7[:, :], T.pI[:, :], 7, OP.bitwise_and, ("pI",), ("p7",))
-    ts(T.pr[:, :], T.gI[:, :], 1, OP.bitwise_and, ("gI",), ("pr",))
-    cp(sc(0), T.gI[:, 0:1], ("gI",), ("s0",))
-    ts(T.ul[:, :], T.p7[:, :], 16, OP.mult, ("p7",), ("ul",))
-    cp(sc(1), T.pr[:, 0:1], ("pr",), ("s1",))
-    ts(sc(2), T.gI[:, 0:1], -320.0, OP.mult, ("gI",), ("s2",), float(CEN), OP.add)
-    ts(sc(3), T.pr[:, 0:1], -4800.0, OP.mult, ("pr",), ("s3",), 4800.0, OP.add)
-    ts(sc(4), T.gI[:, 0:1], -16.0, OP.mult, ("gI",), ("s4",), float(CEN), OP.add)
-    ts(sc(5), T.gI[:, 0:1], 0.0, OP.is_equal, ("gI",), ("s5",), 2560.0, OP.mult)
-    tt(sc(6), sc(2), sc(3), OP.add, ("s2", "s3"), ("s6",))
-    ts(sc(7), sc(2), 4.0, OP.mult, ("s2",), ("s7",))
-    tt(sc(8), sc(4), sc(3), OP.add, ("s3", "s4"), ("s8",))
-    ts(sc(9), sc(8), 320.0, OP.add, ("s8",), ("s9",))
-    ts(sc(10), sc(8), -320.0, OP.add, ("s8",), ("s10",))
-    tt(sc(11), sc(10), sc(5), OP.add, ("s5", "s10"), ("s11",))
-    ts(sc(12), sc(4), float(832 - CEN), OP.add, ("s4",), ("s12",))
-    ts(sc(13), T.pr[:, 0:1], -1.0, OP.mult, ("pr",), ("s13",), 1.0, OP.add)
-    act(T.ivA[:, :], T.idt[:, 0:RING], ("id0",), ("ivA",), bias=320.0)
-    act(T.map[:, CEN - NC:CEN + 2 * NC], T.idt[:, 0:960], ("id0",), ("map0",), bias=float(IDB + CEN - NC))
-    act(T.map[:, 0:NC], T.idt[:, 0:NC], ("id0",), ("map1",), bias=float(IDB))
-    act(T.map[:, INV + CEN - NC:INV + CEN + 2 * NC], T.idt[:, 0:960], ("id0",), ("map2",), scale=0.0)
-    act(T.map[:, INV + WINC - NC:INV + WINC], T.idt[:, 0:NC], ("id0",), ("map3",), scale=0.0)
-    act(T.ivB[:, :], T.idt[:, 0:RING], ("id0",), ("ivB",), bias=float(DBL + 320))
-    act(T.ivC[:, :], T.idt[:, 0:RING], ("id0",), ("ivC",), bias=float(2 * DBL + 320))
-    act(T.src[:, IDB + CEN - NC:IDB + CEN + 2 * NC], T.idt[:, 0:960], ("id0",), ("src0",), scale=4.0, bias=float(4 * (CEN - NC)))
-    act(T.src[:, IDB:IDB + NC], T.idt[:, 0:NC], ("id0",), ("src1",), scale=4.0)
-    mapt = ("map0", "map1", "map2", "map3")
 
-    ts(T.xu[:, 0:52], T.ri[:, 0:52], sc(2), OP.add, rit(0) + rit(1) + ("s2",), ("xu0",))
-    ts(T.xu[:, 52:78], T.ri[:, 52:78], sc(6), OP.add, rit(2) + ("s6",), ("xu1",))
-    cp(T.eu[:, :], T.ri[:, 0:78], rit(0) + rit(1) + rit(2), ("eu",))
-    ts(T.xu[:, 78:130], T.ri[:, 78:130], sc(2), OP.add, rit(3) + rit(4) + ("s2",), ("xu2",))
-    for k, nm in enumerate(("ivA", "ivB", "ivC")):
-        op("V", lambda: g.vector.tensor_copy(T.map[:, 0:2 * WINC].indirect(T.xu[:, 26 * k:26 * k + 26]), T[nm][:, :]), (nm, "xu0", "xu1"), mapt)
-        if k == 0:
-            quant(T.qx, T.sx, 0, NC, T.win, 4 * CEN, ("xO", "xG"), ("qxO", "qxG"))
-            quant(T.qu, T.su, 0, 128, T.ut, 0, ("ut",), ("qu",))
-        if k == 1:
-            op("V", lambda: g.vector.tensor_copy(T.qu2[:, 0:128].bitcast(dt.uint32), T.qu[:, 0:128].bitcast(dt.uint32).indirect(T.ul[:, 0:8])), ("qu", "ul"), ("qu2",))
-            op("V", lambda: g.vector.tensor_copy(T.su2[:, 0:128], T.su[:, 0:128].indirect(T.ul[:, 0:8])), ("qu", "ul"), ("su2",))
+    l1t = tuple(("l1", h) for h in range(8)) + ("l2a", "l2b")
+    ts(T.xu[:, 0:26], T.ri[:, 78:104], sc(2), OP.add, l1t + ("s2",), ("xu0",))
+    ts(T.xu[:, 26:52], T.ri[:, 104:130], sc(14), OP.add, l1t + ("s14",), ("xu1",))
+
+    def scatter(k, nm):
+        op("V", lambda: g.vector.tensor_copy(T.map[:, 0:2 * WINC].indirect(T.xu[:, 26 * k:26 * k + 26]), T[nm][:, :]), (nm, "xu%d" % k), mapt)
+    scatter(0, "iv1")
+    fill(T.ft[:, :], 0.0, ("ft0", "ft1", "ft2"))
+    cp(T.eu[:, :], T.ri[:, 0:78], qtok, ("eu",))
+    quant(T.qu, T.su, 0, 128, T.ut, 0, ("ut",), ("qu",))
+    scatter(1, "iv2")
+    quant(T.qx, T.sx, 0, NC, T.win, 4 * CEN, ("xO", "xG"), ("qxO", "qxG"))
+    op("V", lambda: g.vector.tensor_copy(T.qu2[:, 0:128].bitcast(dt.uint32), T.qu[:, 0:128].bitcast(dt.uint32).indirect(T.ul[:, 0:8])), ("qu", "ul"), ("qu2",))
+    op("V", lambda: g.vector.tensor_copy(T.su2[:, 0:128], T.su[:, 0:128].indirect(T.ul[:, 0:8])), ("qu", "ul"), ("su2",))
+    ts(T.xk[:, :], T.kl[:, :], sc(2), OP.add, klt + ("s2",), ("xk",))
+    ts(T.xe[:, 0:20], T.j20[:, :], sc(17), OP.add, ("j20", "s17"), ("xe0",))
+    ts(T.xe[:, 20:40], T.j20[:, :], sc(18), OP.add, ("j20", "s18"), ("xe1",))
+    act(T.src[:, IDB + CEN - NC:IDB + CEN + 2 * NC], T.idt[:, 0:960], ("id0", "id1"), ("src0",), scale=4.0, bias=float(4 * (CEN - NC)))
+    act(T.src[:, IDB:IDB + NC], T.idt[:, 0:NC], ("id0",), ("src1",), scale=4.0)
     for k in range(3):
         act(T.src[:, DBL * k:DBL * k + 320], T.idt[:, 0:2560].indirect(T.eu[:, 26 * k + 6:26 * k + 26]), ("id0", "id1", "eu", "s7"), (("sr", k, 0),), scale=4.0, bias=sc(7))
         act(T.src[:, DBL * k + 320:DBL * k + 736], T.idt[:, 0:2560].indirect(T.eu[:, 26 * k:26 * k + 26]), ("id0", "id1", "eu", "s7"), (("sr", k, 1),), scale=4.0, bias=sc(7))
     srct = ("src0", "src1") + tuple(("sr", k, i) for k in range(3) for i in range(2))
-    ts(T.ji[:, :], T.ji[:, :], 15, OP.bitwise_and, ("ji",), ("ji",))
-    ts(T.mask[:, :], T.ji[:, :], 0.0, OP.is_equal, ("ji",), ("mask",))
-    ts(T.su3[:, 0:20], T.j20[:, :], sc(8), OP.add, ("j20", "s8"), ("u0",))
-    ts(T.su3[:, 20:40], T.j20[:, :], sc(9), OP.add, ("j20", "s9"), ("u1",))
-    ts(T.su3[:, 40:60], T.j20[:, :], sc(11), OP.add, ("j20", "s11"), ("u2",))
 
-    def look(k, off, n, r, out, w):
-        m, s = T["hm%d" % (k % 2)], T["hs%d" % (k % 2)]
-        tt(m[:, 0:n], T.map[:, 0:2 * WINC].indirect(off), T.mask[:, 0:n], OP.mult, mapt + ("mask",) + r, (("hm", k % 2),))
-        scan(s[:, 0:n], T.keep[:, 0:n], m[:, 0:n], ("keep", ("hm", k % 2)), (("hs", k % 2),))
-        cp(out, s[:, 15:n:16], (("hs", k % 2),), w)
+    def look(k, off, r):
+        m, s = T["hm%d" % k], T["hs%d" % k]
+        tt(m[:, :], T.map[:, 0:2 * WINC].indirect(off), T.mask[:, :], OP.mult, mapt + ("mask",) + r, (("hm", k),))
+        scan(s[:, :], T.keep[:, :], m[:, :], ("keep", ("hm", k)), (("hs", k),))
+
+    def compare(t):
+        ts(T.ft[:, t:192:4], ps[t][:, 0:48], 0.0, OP.is_gt, (("ps", t),), ("ft%d" % t,))
 
     def counts_a():
         mm(ps[0][:, 0:128], T.qx, T.sx, 192, T.qu2, T.su2, 0, 128, ("qxO", "qu2", "su2"), (("ps", 0),))
@@ -292,88 +311,86 @@ def rank_program(g, core, T, topo):
     def counts_b():
         mm(ps[1][:, 0:128], T.qx, T.sx, 0, T.qu2, T.su2, 0, 128, ("qxG", "qu2", "su2"), (("ps", 1),))
         mm(ps[2][:, 0:128], T.qx, T.sx, 64, T.qu2, T.su2, 0, 128, ("qxO", "qxG", "qu2", "su2"), (("ps", 2),))
-        for t in range(3):
-            ts(T.ft[:, t:192:4], ps[t][:, 0:48], 0.0, OP.is_gt, (("ps", t),), ("ft%d" % t,))
+        compare(1)
+        compare(2)
         quant(T.qf, T.sf, 0, 128, T.ft, 0, ("ft0", "ft1", "ft2"), ("qf",))
         mm(ps[3][:, 0:128], T.qc, T.sct, 0, T.qf, T.sf, 0, 128, ("qc", "qf"), (("ps", 3),))
 
-    def counts_c(rd):
+    def counts_c():
         tt(T.cm[:, :], ps[3][:, 0:48], T.mk[:, :], OP.mult, (("ps", 3), "mk"), ("cm",))
         scan(T.cs[:, :], T.kp8[:, :], T.cm[:, :], ("cm", "kp8"), ("cs",))
 
-    quant(T.qc, T.sct, 0, 128, T.ct, 0, tuple(("ct", k) for k in range(5)), ("qc",))
     counts_a()
-    counts_b()
-    ts(T.cst[:, :], T.cst[:, :], sc(1), OP.mult, ("c0", "c1", "c2", "c3", "s1"), ("c0",))
-    tt(T.jj[:, :], T.jj[:, :], T.cst[:, :], OP.subtract, ("jja", "jjb", "c0"), ("jja",))
-    ts(T.jj[:, :], T.jj[:, :], sc(0), OP.subtract, ("jja", "s0"), ("jja",))
-    ts(T.jj[:, :], T.jj[:, :], 7, OP.bitwise_and, ("jja",), ("jja",))
-    ts(T.mk[:, :], T.jj[:, :], 0.0, OP.is_equal, ("jja",), ("mk",))
-
-    look(0, T.su3[:, 20:40], NC, ("u1",), T.pm[:, 0:20], ("pm0",))
-    look(1, T.su3[:, 40:60], NC, ("u2",), T.pm[:, 20:40], ("pm1",))
+    look(0, T.xk[:, :], ("xk",))
+    fill(T.kp8[:, :], 1.0, ("kp8",))
+    fill(T.bA[:, :], float(IDB + CEN), ("bA0", "bA1", "bA2", "bA3"))
+    h0 = ("hs", 0)
+    ts(T.w1[:, :], T.hs0[:, 15:RING:16], float(IDB), OP.is_ge, (h0,), ("w1",), -320.0, OP.mult)
+    ts(T.w2[:, :], T.hs0[:, 15:RING:16], float(IDB), OP.is_ge, (h0, "s25"), ("w2",), sc(25), OP.mult)
+    ts(T.w3[:, :], T.hs0[:, 15:RING:16], float(DBL), OP.add, (h0,), ("w3",))
+    tt(T.ph[:, 0:26], T.hs0[:, 15:RING:16], T.w1[:, :], OP.add, (h0, "w1"), ("ph0",))
+    tt(T.ph[:, 26:52], T.w3[:, :], T.w2[:, :], OP.add, ("w3", "w2"), ("ph1",))
+    cp(T.bA[:, 0:20], T.hs0[:, 15:NC:16], (h0,), ("bA0",))
+    cp(T.bA[:, 20:46], T.hs0[:, 15:RING:16], (h0,), ("bA1",))
     for k, h in enumerate((1, 3, 5, 7)):
         f = (h + 1) % 8
-        dma("Y", "dL", T.lr[GRP * h:GRP * h + GRP, 0:20], T.pm[GRP * (h - 1):GRP * h, 0:20], ("pm0", "lr"), (("lr", k),))
-        dma("Y", "dL", T.lr[GRP * h:GRP * h + GRP, 20:40], T.pm[GRP * f:GRP * f + GRP, 20:40], ("pm1", "lr"), (("lr", 4 + k),))
-    look(0, T.xu[:, 78:104], RING, ("xu2",), T.bA[:, 0:26], ("bA0",))
-    look(1, T.xu[:, 104:130], RING, ("xu2",), T.bA[:, 26:52], ("bA1",))
-    look(0, T.su3[:, 0:20], NC, ("u0",), T.bA[:, 52:72], ("bA2",))
-    bAt = ("bA0", "bA1", "bA2")
-    ts(T.mA[:, 0:26], T.bA[:, 0:26], float(DBL), OP.is_lt, bAt, ("mA",))
-    ts(T.g1[:, :], T.bA[:, :], float(DBL), OP.is_ge, bAt, ("g1",))
-    ts(T.g2[:, :], T.bA[:, :], float(2 * DBL), OP.is_ge, bAt, ("g2",))
-    ts(T.g3[:, :], T.bA[:, :], float(3 * DBL), OP.is_ge, bAt, ("g3",))
-    tt(T.mB[:, :], T.g1[:, :], T.g2[:, :], OP.subtract, ("g1", "g2"), ("mB",))
-    tt(T.mC[:, :], T.g2[:, :], T.g3[:, :], OP.subtract, ("g2", "g3"), ("mC",))
-
-    def even_lists():
-        b = lambda k: T.bt[:, 20 * k:20 * k + 20]
-        lrt = tuple(("lr", k) for k in range(8)) + ("lr",)
-        ts(b(0), T.bA[:, 52:72], sc(13), OP.mult, ("bA2", "s13"), ("b0",))
-        ts(T.j832[:, :], T.j20[:, :], sc(12), OP.add, ("j20", "s12"), ("j832",))
-        tt(b(1), b(0), T.lr[:, 0:20], OP.add, ("b0",) + lrt, ("b1",))
-        ts(T.mE[:, :], T.lr[:, 20:40], 0.0, OP.is_gt, lrt, ("mE",))
-        ts(b(3), T.lr[:, 20:40], float(2 * DBL + 320 - RING), OP.subtract, lrt, ("b3",), 0.0, OP.max)
-        ts(T.mD[:, :], b(1), 0.0, OP.is_gt, ("b1",), ("mD",))
-        ts(b(2), b(1), float(2 * DBL + 320), OP.subtract, ("b1",), ("b2",), 0.0, OP.max)
-        tt(b(4), T.mD[:, :], T.mE[:, :], OP.add, ("mD", "mE"), ("b4",))
-        tt(b(7), b(2), b(3), OP.add, ("b2", "b3"), ("b7",))
-        ts(b(5), b(4), -1.0, OP.mult, ("b4",), ("b5",), 1.0, OP.add)
-        ts(b(9), T.mE[:, :], float(RING), OP.mult, ("mE",), ("b9",))
-        tt(b(6), b(5), T.j832[:, :], OP.mult, ("b5", "j832"), ("b6",))
-        ts(b(8), b(5), -100000.0, OP.mult, ("b5",), ("b8",))
-        tt(T.bB[:, :], b(6), b(7), OP.add, ("b6", "b7"), ("bB",))
-        tt(T.thr[:, :], b(8), b(9), OP.add, ("b8", "b9"), ("thr",))
+        dma("Y", "dL", T.bA[GRP * h:GRP * h + GRP, 20:46], T.ph[GRP * (h - 1):GRP * h, 0:26], ("ph0", "bA1"), (("bh", k),))
+        dma("Y", "dL", T.bA[GRP * h:GRP * h + GRP, 46:72], T.ph[GRP * f:GRP * f + GRP, 26:52], ("ph1", "bA2"), (("bh", 4 + k),))
+    ts(T.rt[:, :], T.hs0[:, NC + 15:640:16], 2.0, OP.mult, (h0, "s23"), ("rt",), sc(23), OP.add)
+    look(1, T.xe[:, :], ("xe0", "xe1"))
+    fill(T.kp8[:, 0:48:8], 0.0, ("kp8",))
+    quant(T.qc, T.sct, 0, 128, T.ct, 0, tuple(("ct", k) for k in range(5)), ("qc",))
+    ts(T.pe[:, :], T.hs1[:, 15:640:16], 2.0, OP.mult, (("hs", 1),), ("pe",))
+    for k, h in enumerate((1, 3, 5, 7)):
+        e, f = (h + 1) % 8, (h + 2) % 8
+        dma("Y", "dE", T.lt[GRP * e:GRP * e + GRP, :], T.pe[GRP * h:GRP * h + GRP, 0:20], ("pe",), (("lt", k),))
+        dma("Y", "dE", T.lt[GRP * f:GRP * f + GRP, :], T.pe[GRP * h:GRP * h + GRP, 20:40], ("pe",), (("lt", 4 + k),))
+    compare(0)
+    counts_b()
+    ts(T.cst[:, :], T.cst[:, :], sc(1), OP.mult, ("c0", "c1", "c2", "c3", "s1"), ("c0",))
+    ts(T.j832[:, :], T.j20[:, :], sc(12), OP.add, ("j20", "s12"), ("j832",))
+    tt(T.jj[:, :], T.jj[:, :], T.cst[:, :], OP.subtract, ("jja", "jjb", "c0"), ("jja",))
+    tt(T.te[:, :], T.rt[:, :], T.j832[:, :], OP.min, ("rt", "j832"), ("te",))
+    ts(T.jj[:, :], T.jj[:, :], sc(0), OP.subtract, ("jja", "s0"), ("jja",))
+    ts(T.mR[:, 72:92], T.rt[:, :], 832.0, OP.is_lt, ("rt",), ("mE",), 2.0, OP.mult)
+    ts(T.jj[:, :], T.jj[:, :], 7, OP.bitwise_and, ("jja",), ("jja",))
+    for b in range(2):
+        quant(T.qe, T.se, 128 * b, 128 * b + 128, T.e1, 3 - b, ("e1",), (("qe", b),))
+    ts(T.mk[:, :], T.jj[:, :], 0.0, OP.is_equal, ("jja",), ("mk",))
+    for b in range(2, 4):
+        quant(T.qe, T.se, 128 * b, 128 * b + 128, T.e1, 3 - b, ("e1",), (("qe", b),))
+    bAt = ("bA0", "bA1", "bA2") + tuple(("bh", k) for k in range(8))
+    ts(T.g1[:, :], T.bA[:, 0:72], float(DBL), OP.is_ge, bAt, ("g1",))
+    ts(T.g2[:, :], T.bA[:, 0:72], float(2 * DBL), OP.is_ge, bAt, ("g2",))
+    ts(T.g3[:, :], T.bA[:, 0:72], float(3 * DBL), OP.is_ge, bAt, ("g3",))
+    ts(T.mR[:, 20:46], T.bA[:, 20:46], float(DBL), OP.is_lt, bAt, ("mA",))
+    tt(T.mL[:, 0:72], T.g1[:, :], T.g2[:, :], OP.subtract, ("g1", "g2"), ("mB",))
+    tt(T.mR[:, 46:72], T.g2[:, 46:72], T.g3[:, 46:72], OP.subtract, ("g2", "g3"), ("mC",))
+    ltt = tuple(("lt", k) for k in range(8))
+    ts(T.mL[:, 72:92], T.lt[:, :], 832.0, OP.is_lt, ltt, ("mD",), 2.0, OP.mult)
+    tt(T.bA[:, 72:92], T.lt[:, :], T.te[:, :], OP.min, ltt + ("te",), ("bA3",))
 
     cs = lambda k: T.cs[:, 8 * k + 7:8 * k + 8]
-    SPL = 44
 
-    def lists_a():
-        ts(T.ta[:, :], T.mB[:, :], cs(0), OP.mult, ("mB", "cs"), ("ta",))
-        ts(T.tb[:, 0:26], T.mA[:, 0:26], cs(2), OP.mult, ("mA", "cs"), ("tb0",))
-        ts(T.tb[:, 26:52], T.mC[:, 26:52], cs(4), OP.mult, ("mC", "cs"), ("tb1",))
-        tt(T.tc[:, :], T.bA[:, :], T.ta[:, :], OP.subtract, bAt + ("ta",), ("tc",))
-        tt(T.tc[:, 0:52], T.tc[:, 0:52], T.tb[:, 0:52], OP.subtract, ("tc", "tb0", "tb1"), ("tc",))
-        cp(T.oA[:, :], T.tc[:, :], ("tc",), ("oA",))
-        act(T.tab[:, 0:16 * SPL], T.src[:, :].indirect(T.oA[:, 0:SPL]), srct + ("oA",), ("tab0",))
-
-    def lists_b():
-        ts(T.td[:, :], T.mD[:, :], cs(1), OP.mult, ("mD", "cs"), ("td",))
-        ts(T.te[:, :], T.mE[:, :], cs(3), OP.mult, ("mE", "cs"), ("te",))
-        tt(T.tt[:, :], T.bB[:, :], T.td[:, :], OP.subtract, ("bB", "td"), ("tt",))
-        tt(T.tt[:, :], T.tt[:, :], T.te[:, :], OP.subtract, ("tt", "te"), ("tt",))
-        tt(T.tw[:, :], T.tt[:, :], T.thr[:, :], OP.is_lt, ("tt", "thr"), ("tw",))
-        ts(T.tw[:, :], T.tw[:, :], float(RING), OP.mult, ("tw",), ("tw",))
-        tt(T.tt[:, :], T.tt[:, :], T.tw[:, :], OP.add, ("tt", "tw"), ("tt",))
-        cp(T.oB[:, :], T.tt[:, :], ("tt",), ("oB",))
-
-    def lists_c():
-        cp(T.tab[:, 16 * SPL:1152], T.src[:, :].indirect(T.oA[:, SPL:72]), srct + ("oA",), ("tab1",))
+    def lists():
+        ts(T.ta[:, 0:72], T.mL[:, 0:72], cs(0), OP.mult, ("mB", "cs"), ("ta0",))
+        ts(T.tb[:, 20:46], T.mR[:, 20:46], cs(2), OP.mult, ("mA", "cs"), ("tb0",))
+        ts(T.tb[:, 46:72], T.mR[:, 46:72], cs(4), OP.mult, ("mC", "cs"), ("tb1",))
+        ts(T.ta[:, 72:92], T.mL[:, 72:92], cs(1), OP.mult, ("mD", "cs"), ("ta1",))
+        ts(T.tb[:, 72:92], T.mR[:, 72:92], cs(3), OP.mult, ("mE", "cs"), ("tb2",))
+        tt(T.tq[:, :], T.bA[:, :], T.ta[:, :], OP.subtract, bAt + ("bA3", "ta0", "ta1"), ("tq",))
+        tt(T.tq[:, 20:92], T.tq[:, 20:92], T.tb[:, 20:92], OP.subtract, ("tq", "tb0", "tb1", "tb2"), ("tq",))
+        cp(T.oA[:, :], T.tq[:, 0:72], ("tq",), ("oA",))
+        act(T.tab[:, 0:832:2], T.src[:, :].indirect(T.oA[:, 20:46]), srct + ("oA",), ("tab0",))
+        act(T.tab[:, 1:832:2], T.src[:, :].indirect(T.oA[:, 46:72]), srct + ("oA",), ("tab1",))
+        ts(T.tw[:, :], T.tq[:, 72:92], 0.0, OP.is_lt, ("tq",), ("tw",), 832.0, OP.mult)
+        cp(T.tab[:, 832:1152], T.src[:, :].indirect(T.oA[:, 0:20]), srct + ("oA",), ("tab2",))
+        tt(T.tw[:, :], T.tq[:, 72:92], T.tw[:, :], OP.add, ("tq", "tw"), ("tw",))
+        cp(T.oB[:, :], T.tw[:, :], ("tw",), ("oB",))
 
     def turn(h, tile, tok):
         m, s = T.bm[:, HALF * h:HALF * h + HALF], T.bs
-        tt(m, T.tab[:, :].indirect(T.oB[:, 10 * h:10 * h + 10]), T.mask[:, 0:HALF], OP.mult, ("tab0", "tab1", "oB", "mask"), (("bm", h),))
+        tt(m, T.tab[:, :].indirect(T.oB[:, 10 * h:10 * h + 10]), T.mask[:, 0:HALF], OP.mult, ("tab0", "tab1", "tab2", "oB", "mask"), (("bm", h),))
         scan(s[:, HALF * h:HALF * h + HALF], T.keep[:, 0:HALF], m, ("keep", ("bm", h)), (("bs", h),))
         for t in (2, 0, 3, 1):
             c = 40 * h + 10 * t
@@ -407,19 +424,9 @@ def rank_program(g, core, T, topo):
 
     for rd in range(3):
         last = rd == 2
-        counts_c(rd)
-        if rd == 0:
-            lists_a()
-            even_lists()
-        else:
-            lists_a()
-        lists_b()
-        lists_c()
+        counts_c()
+        lists()
         turn(0, T.gr, "gr")
-        if rd == 0:
-            act(T.e32[:, :], T.e1[:, :], ("e1",), ("e32",), scale=32.0)
-            for b in range(4):
-                quant(T.qe, T.se, 128 * b, 128 * b + 128, T.e1, 3 - b, ("e1",), (("qe", b),))
         quant(T.q1, T.s1, 0, HALF, T.gr, 0, four("gr"), ("q1",))
         unpack(T.q1, T.s1, ("q1",), 4, T.gt, "gt")
         quant(T.q2, T.s2, 0, HALF, T.gt, 0, four("gt"), ("q2",))
@@ -436,16 +443,17 @@ def rank_program(g, core, T, topo):
         land = ("land", rd)
         writer[land] = [(arr, 2 * ne, {}, "R")]
         if rd == 0:
-            for b in range(4):
-                quant(T.qe, T.se, 512 + 128 * b, 640 + 128 * b, T.e32, 3 - b, ("e32",), (("qe", 4 + b),))
+            act(T.e32[:, :], T.e1[:, :], ("e1",), ("e32",), scale=32.0)
         turn(1, T.ow, "ow")
         quant(T.qo, T.so, 0, HALF, T.ow, 0, four("ow"), ("qo",))
+        if rd == 0:
+            for b in range(4):
+                quant(T.qe, T.se, 512 + 128 * b, 640 + 128 * b, T.e32, 3 - b, ("e32",), (("qe", 4 + b),))
         unpack(T.qo, T.so, ("qo",), 0, T.zo, "zo")
         first(0, T.qo, T.so, ("qo",))
         quant(T.qzo, T.szo, 0, HALF, T.zo, 0, four("zo"), ("qzo",))
         layer(0, T.qzo, T.szo, ("qzo",), 4 * (CEN + HALF), "xo")
-        for t in ("xO",):
-            writer[t], reader[t] = sum([writer[("xo", b)] for b in range(4)], []), []
+        writer["xO"], reader["xO"] = sum([writer[("xo", b)] for b in range(4)], []), []
         if not last:
             gate("Y", ("xO",), tuple(("shO", k) for k in range(NSH)))
             for k, (p0, p1, q0, c, n) in enumerate(shifts(HALF, NC)):
@@ -467,9 +475,10 @@ def rank_program(g, core, T, topo):
         unpack(T["lc%d" % rd], T["ls%d" % rd], (land,), 4, T.zg, "zg")
         first(4, T["lc%d" % rd], T["ls%d" % rd], (land,))
         quant(T.qzg, T.szg, 0, HALF, T.zg, 0, four("zg"), ("qzg",))
+        if not last:
+            compare(0)
         layer(4, T.qzg, T.szg, ("qzg",), 4 * CEN, "xg")
-        for t in ("xG",):
-            writer[t], reader[t] = sum([writer[("xg", b)] for b in range(4)], []), []
+        writer["xG"], reader["xG"] = sum([writer[("xg", b)] for b in range(4)], []), []
         if not last:
             gate("Y", ("xG",), tuple(("shG", k) for k in range(NSH)))
             for k, (p0, p1, q0, c, n) in enumerate(shifts(0, HALF)):

@@ -214,6 +214,8 @@ def rank_program(g, core, T, topo):
     op("G", lambda: g.iota(T.jj[:, 0:40], [[1, 5], [1, 8]], 63, 0), (), ("jja",))
     op("G", lambda: g.iota(T.jj[:, 40:48], [[1, 8]], 64, 0), (), ("jjb",))
     op("G", lambda: g.iota(T.idt[:, RING:2560], [[1, 2560 - RING]], RING, 0, **fl), (), ("id1",))
+    op("G", lambda: g.iota(T.ew[:, :], [[0, 516]], 32, 0, **fl), (), ("ew",))
+    op("G", lambda: g.affine_select(T.e1[:, :], T.ew[:, :], [[1, 516]], OP.is_equal, 0.0, -3, -4), ("ew",), ("e1",))
     ts(T.gI[:, :], T.pI[:, :], 4, OP.arith_shift_right, ("pI",), ("gI",))
     ts(T.kI[:, :], T.pI[:, :], 15, OP.bitwise_and, ("pI",), ("kI",))
     ts(T.p7[:, :], T.pI[:, :], 7, OP.bitwise_and, ("pI",), ("p7",))
@@ -261,13 +263,9 @@ def rank_program(g, core, T, topo):
     act(T.mask[:, :], T.jd[:, :], ("jd",), ("mask",), scale=-1.0, bias=1.0, fn=FN.Relu)
     act(T.keep[:, :], T.jm[:, :], ("jm",), ("keep",), fn=FN.Sign)
     mapt = tuple("map%d" % k for k in range(4))
-    fill(T.ew[:, :], 1.0, ("ew",))
-    op("G", lambda: g.affine_select(T.e1[:, :], T.ew[:, :], [[1, 516]], OP.is_equal, 0.0, -3, -4), ("ew",), ("e1",))
-    fill(T.ct[:, 0:512:4], 1.0, (("ct", 0),))
-    fill(T.ct[:, 1:512:4], 1.0, (("ct", 1),))
-    fill(T.ct[0:64, 2:512:4], 0.0, (("ct", 2),))
-    fill(T.ct[64:128, 2:512:4], 1.0, (("ct", 3),))
-    fill(T.ct[:, 3:512:4], 0.0, (("ct", 4),))
+    for k, (p0, p1, t, c) in enumerate(((0, 128, 0, 1.0), (0, 128, 1, 1.0), (0, 64, 2, 0.0), (64, 128, 2, 1.0), (0, 128, 3, 0.0))):
+        act(T.ct[p0:p1, t:512:4], T.idt[p0:p1, 0:128], ("id0",), (("ct", k),), scale=0.0, bias=c)
+    act(T.ft[:, :], T.jm[:, 0:512], ("jm",), ("ft0", "ft1", "ft2"), scale=0.0)
     fill(T.cst[:, 0:24], -1, ("c0",))
     fill(T.cst[:, 24:32], 3, ("c1",))
     fill(T.cst[:, 32:40], 5, ("c2",))
@@ -280,7 +278,6 @@ def rank_program(g, core, T, topo):
     def scatter(k, nm):
         op("V", lambda: g.vector.tensor_copy(T.map[:, 0:2 * WINC].indirect(T.xu[:, 26 * k:26 * k + 26]), T[nm][:, :]), (nm, "xu%d" % k), mapt)
     scatter(0, "iv1")
-    fill(T.ft[:, :], 0.0, ("ft0", "ft1", "ft2"))
     cp(T.eu[:, :], T.ri[:, 0:78], qtok, ("eu",))
     quant(T.qu, T.su, 0, 128, T.ut, 0, ("ut",), ("qu",))
     scatter(1, "iv2")
@@ -311,8 +308,8 @@ def rank_program(g, core, T, topo):
     def counts_b():
         mm(ps[1][:, 0:128], T.qx, T.sx, 0, T.qu2, T.su2, 0, 128, ("qxG", "qu2", "su2"), (("ps", 1),))
         mm(ps[2][:, 0:128], T.qx, T.sx, 64, T.qu2, T.su2, 0, 128, ("qxO", "qxG", "qu2", "su2"), (("ps", 2),))
-        compare(1)
-        compare(2)
+        for t in range(3):
+            compare(t)
         quant(T.qf, T.sf, 0, 128, T.ft, 0, ("ft0", "ft1", "ft2"), ("qf",))
         mm(ps[3][:, 0:128], T.qc, T.sct, 0, T.qf, T.sf, 0, 128, ("qc", "qf"), (("ps", 3),))
 
@@ -345,7 +342,6 @@ def rank_program(g, core, T, topo):
         e, f = (h + 1) % 8, (h + 2) % 8
         dma("Y", "dE", T.lt[GRP * e:GRP * e + GRP, :], T.pe[GRP * h:GRP * h + GRP, 0:20], ("pe",), (("lt", k),))
         dma("Y", "dE", T.lt[GRP * f:GRP * f + GRP, :], T.pe[GRP * h:GRP * h + GRP, 20:40], ("pe",), (("lt", 4 + k),))
-    compare(0)
     counts_b()
     ts(T.cst[:, :], T.cst[:, :], sc(1), OP.mult, ("c0", "c1", "c2", "c3", "s1"), ("c0",))
     ts(T.j832[:, :], T.j20[:, :], sc(12), OP.add, ("j20", "s12"), ("j832",))
@@ -367,34 +363,38 @@ def rank_program(g, core, T, topo):
     tt(T.mL[:, 0:72], T.g1[:, :], T.g2[:, :], OP.subtract, ("g1", "g2"), ("mB",))
     tt(T.mR[:, 46:72], T.g2[:, 46:72], T.g3[:, 46:72], OP.subtract, ("g2", "g3"), ("mC",))
     ltt = tuple(("lt", k) for k in range(8))
-    ts(T.mL[:, 72:92], T.lt[:, :], 832.0, OP.is_lt, ltt, ("mD",), 2.0, OP.mult)
-    tt(T.bA[:, 72:92], T.lt[:, :], T.te[:, :], OP.min, ltt + ("te",), ("bA3",))
 
     cs = lambda k: T.cs[:, 8 * k + 7:8 * k + 8]
 
     def lists():
         ts(T.ta[:, 0:72], T.mL[:, 0:72], cs(0), OP.mult, ("mB", "cs"), ("ta0",))
-        ts(T.tb[:, 20:46], T.mR[:, 20:46], cs(2), OP.mult, ("mA", "cs"), ("tb0",))
-        ts(T.tb[:, 46:72], T.mR[:, 46:72], cs(4), OP.mult, ("mC", "cs"), ("tb1",))
+        act(T.tb[:, 46:72], T.mR[:, 46:72], ("mC", "cs"), ("tb1",), scale=cs(4))
+        act(T.tb[:, 72:92], T.mR[:, 72:92], ("mE", "cs"), ("tb2",), scale=cs(3))
         ts(T.ta[:, 72:92], T.mL[:, 72:92], cs(1), OP.mult, ("mD", "cs"), ("ta1",))
-        ts(T.tb[:, 72:92], T.mR[:, 72:92], cs(3), OP.mult, ("mE", "cs"), ("tb2",))
+        ts(T.tb[:, 20:46], T.mR[:, 20:46], cs(2), OP.mult, ("mA", "cs"), ("tb0",))
         tt(T.tq[:, :], T.bA[:, :], T.ta[:, :], OP.subtract, bAt + ("bA3", "ta0", "ta1"), ("tq",))
         tt(T.tq[:, 20:92], T.tq[:, 20:92], T.tb[:, 20:92], OP.subtract, ("tq", "tb0", "tb1", "tb2"), ("tq",))
         cp(T.oA[:, :], T.tq[:, 0:72], ("tq",), ("oA",))
         act(T.tab[:, 0:832:2], T.src[:, :].indirect(T.oA[:, 20:46]), srct + ("oA",), ("tab0",))
-        act(T.tab[:, 1:832:2], T.src[:, :].indirect(T.oA[:, 46:72]), srct + ("oA",), ("tab1",))
+        act(T.tab[:, 1:512:2], T.src[:, :].indirect(T.oA[:, 46:62]), srct + ("oA",), ("tab1",))
         ts(T.tw[:, :], T.tq[:, 72:92], 0.0, OP.is_lt, ("tq",), ("tw",), 832.0, OP.mult)
         cp(T.tab[:, 832:1152], T.src[:, :].indirect(T.oA[:, 0:20]), srct + ("oA",), ("tab2",))
+        cp(T.tab[:, 513:832:2], T.src[:, :].indirect(T.oA[:, 62:72]), srct + ("oA",), ("tab3",))
         tt(T.tw[:, :], T.tq[:, 72:92], T.tw[:, :], OP.add, ("tq", "tw"), ("tw",))
         cp(T.oB[:, :], T.tw[:, :], ("tw",), ("oB",))
 
-    def turn(h, tile, tok):
-        m, s = T.bm[:, HALF * h:HALF * h + HALF], T.bs
-        tt(m, T.tab[:, :].indirect(T.oB[:, 10 * h:10 * h + 10]), T.mask[:, 0:HALF], OP.mult, ("tab0", "tab1", "tab2", "oB", "mask"), (("bm", h),))
-        scan(s[:, HALF * h:HALF * h + HALF], T.keep[:, 0:HALF], m, ("keep", ("bm", h)), (("bs", h),))
+    def pick(h):
+        tt(T.bm[:, HALF * h:HALF * h + HALF], T.tab[:, :].indirect(T.oB[:, 10 * h:10 * h + 10]), T.mask[:, 0:HALF], OP.mult, ("tab0", "tab1", "tab2", "tab3", "oB", "mask"), (("bm", h),))
+
+    def fold(h):
+        scan(T.bs[:, HALF * h:HALF * h + HALF], T.keep[:, 0:HALF], T.bm[:, HALF * h:HALF * h + HALF], ("keep", ("bm", h)), (("bs", h),))
+
+    def offsets(h):
         for t in (2, 0, 3, 1):
             c = 40 * h + 10 * t
-            ts(T.l4[:, c:c + 10], s[:, HALF * h + 15:HALF * h + HALF:16], float(t), OP.add, (("bs", h),), (("l4", h, t),))
+            ts(T.l4[:, c:c + 10], T.bs[:, HALF * h + 15:HALF * h + HALF:16], float(t), OP.add, (("bs", h),), (("l4", h, t),))
+
+    def gather(h, tile, tok):
         wt = ("xO", "xG") + tuple((n, k) for n in ("shO", "shG") for k in range(NSH))
         for t in (2, 0, 3, 1):
             c = 40 * h + 10 * t
@@ -404,15 +404,19 @@ def rank_program(g, core, T, topo):
             else:
                 cp(tile[:, t:4 * HALF:4], src, wt + (("l4", h, t),), ((tok, t),))
 
-    def unpack(q, s, qt, base, tile, tok):
+    def unpack(q, s, qt, base, tile, tok, beside=()):
         for b in range(4):
             mm(ps[base + b][:, 0:HALF], T.qe, T.se, 128 * b, q, s, 0, HALF, (("qe", b),) + qt, (("ps", base + b),))
         for b in range(4):
-            evac("VS"[b % 2], tile[:, b:4 * HALF:4], ps[base + b][:, 0:HALF], (("ps", base + b),), ((tok, b),), 1.0)
+            if b % 2 == 0 and beside:
+                beside[b // 2]()
+            evac("VS"[b % 2], tile[:, b:4 * HALF:4], ps[base + b][:, 0:HALF], (("ps", base + b),), ((tok, b),), 2.0 ** -5)
+        if beside:
+            beside[2]()
 
     def first(base, q, s, qt):
         for b in range(4):
-            mm(ps[base + b][:, 0:HALF], T.qe, T.se, 512 + 128 * b, q, s, 0, HALF, (("qe", 4 + b),) + qt, (("ps", base + b),), True, False)
+            mm(ps[base + b][:, 0:HALF], T.qe, T.se, 128 * b, q, s, 0, HALF, (("qe", b),) + qt, (("ps", base + b),), True, False)
 
     def layer(base, q, s, qt, c0, tok):
         for b in range(4):
@@ -425,10 +429,16 @@ def rank_program(g, core, T, topo):
     for rd in range(3):
         last = rd == 2
         counts_c()
+        if rd == 0:
+            ts(T.mL[:, 72:92], T.lt[:, :], 832.0, OP.is_lt, ltt, ("mD",), 2.0, OP.mult)
+            tt(T.bA[:, 72:92], T.lt[:, :], T.te[:, :], OP.min, ltt + ("te",), ("bA3",))
         lists()
-        turn(0, T.gr, "gr")
+        pick(0)
+        fold(0)
+        offsets(0)
+        gather(0, T.gr, "gr")
         quant(T.q1, T.s1, 0, HALF, T.gr, 0, four("gr"), ("q1",))
-        unpack(T.q1, T.s1, ("q1",), 4, T.gt, "gt")
+        unpack(T.q1, T.s1, ("q1",), 4, T.gt, "gt", (lambda: pick(1), lambda: fold(1), lambda: offsets(1)))
         quant(T.q2, T.s2, 0, HALF, T.gt, 0, four("gt"), ("q2",))
         dst = T.cores[rank ^ MASKS[rd]]
         rid, pid = topo.addr(dst)[0], topo.addr(dst)[1]
@@ -442,13 +452,8 @@ def rank_program(g, core, T, topo):
         mark("G", "sent", total["sent"], ("q2",), ())
         land = ("land", rd)
         writer[land] = [(arr, 2 * ne, {}, "R")]
-        if rd == 0:
-            act(T.e32[:, :], T.e1[:, :], ("e1",), ("e32",), scale=32.0)
-        turn(1, T.ow, "ow")
+        gather(1, T.ow, "ow")
         quant(T.qo, T.so, 0, HALF, T.ow, 0, four("ow"), ("qo",))
-        if rd == 0:
-            for b in range(4):
-                quant(T.qe, T.se, 512 + 128 * b, 640 + 128 * b, T.e32, 3 - b, ("e32",), (("qe", 4 + b),))
         unpack(T.qo, T.so, ("qo",), 0, T.zo, "zo")
         first(0, T.qo, T.so, ("qo",))
         quant(T.qzo, T.szo, 0, HALF, T.zo, 0, four("zo"), ("qzo",))
@@ -458,10 +463,15 @@ def rank_program(g, core, T, topo):
             gate("Y", ("xO",), tuple(("shO", k) for k in range(NSH)))
             for k, (p0, p1, q0, c, n) in enumerate(shifts(HALF, NC)):
                 dma("Y", "shO", T.win[p0:p1, c:c + n], T.win[q0:q0 + p1 - p0, 4 * (CEN + HALF):4 * (CEN + NC)], ("xO",), (("shO", k),))
+        unpack(T["lc%d" % rd], T["ls%d" % rd], (land,), 4, T.zg, "zg")
+        first(4, T["lc%d" % rd], T["ls%d" % rd], (land,))
+        quant(T.qzg, T.szg, 0, HALF, T.zg, 0, four("zg"), ("qzg",))
         quant(T.qx, T.sx, HALF, NC, T.win, 4 * (CEN + HALF), ("xO",), ("qxO",))
         act(T.acs[:, rd:rd + 1], cs(5), ("cs",), (("ac", rd),))
         if rd == 0:
             quant(T.qv, T.sv, 0, 128, T.vt, 0, ("vt",), ("qv",))
+        layer(4, T.qzg, T.szg, ("qzg",), 4 * CEN, "xg")
+        writer["xG"], reader["xG"] = sum([writer[("xg", b)] for b in range(4)], []), []
         if last:
             dma("Y", "dOut", T.oc[:, 4 * HALF:4 * NC], T.qx[:, HALF:NC].bitcast(dt.uint8), ("qxO",), ("oco",))
             for k in range(4):
@@ -472,13 +482,6 @@ def rank_program(g, core, T, topo):
             dma("Y", "dOut", T.y[:, HALF:NC], T.yt[:, HALF:NC], ("yO",), ("you",))
         else:
             counts_a()
-        unpack(T["lc%d" % rd], T["ls%d" % rd], (land,), 4, T.zg, "zg")
-        first(4, T["lc%d" % rd], T["ls%d" % rd], (land,))
-        quant(T.qzg, T.szg, 0, HALF, T.zg, 0, four("zg"), ("qzg",))
-        if not last:
-            compare(0)
-        layer(4, T.qzg, T.szg, ("qzg",), 4 * CEN, "xg")
-        writer["xG"], reader["xG"] = sum([writer[("xg", b)] for b in range(4)], []), []
         if not last:
             gate("Y", ("xG",), tuple(("shG", k) for k in range(NSH)))
             for k, (p0, p1, q0, c, n) in enumerate(shifts(0, HALF)):

import numpy as np
from concourse.mybir import dt, AluOpType, ActivationFunctionType

N = 4
MASKS = (1, 2, 3)
NC, HALF, GRP, RING, DBL = 320, 160, 16, 416, 736
CEN = 7 * NC
WINC = 15 * NC
IDB = 3 * DBL
INV = WINC
ABS = 2500
OP = AluOpType
FN = ActivationFunctionType

SCRATCH = {
    "win": ("sbuf", [128, 4 * WINC], "bfloat16"),
    "map": ("sbuf", [128, 2 * WINC], "float32"),
    "src": ("sbuf", [128, IDB + WINC], "float32"),
    "idt": ("sbuf", [128, 2560], "float32"),
    "iv1": ("sbuf", [128, RING], "float32"), "iv2": ("sbuf", [128, RING], "float32"),
    "ri": ("sbuf", [128, 130], "int32"), "eu": ("sbuf", [128, 78], "uint16"), "xu": ("sbuf", [128, 52], "uint16"),
    "kl": ("sbuf", [128, 40], "int32"), "xk": ("sbuf", [128, 40], "uint16"), "xe": ("sbuf", [128, 40], "uint16"),
    "pI": ("sbuf", [128, 8], "int32"), "gI": ("sbuf", [128, 8], "int32"), "pr": ("sbuf", [128, 8], "int32"), "p7": ("sbuf", [128, 8], "int32"),
    "kI": ("sbuf", [128, 8], "int32"), "ul": ("sbuf", [128, 8], "uint16"),
    "sc": ("sbuf", [128, 32], "float32"),
    "jj": ("sbuf", [128, 48], "int32"), "cst": ("sbuf", [128, 48], "int32"), "mk": ("sbuf", [128, 48], "float32"), "kp8": ("sbuf", [128, 48], "float32"),
    "jm": ("sbuf", [128, 640], "float32"), "jd": ("sbuf", [128, 640], "float32"), "mask": ("sbuf", [128, 640], "float32"), "keep": ("sbuf", [128, 640], "float32"),
    "j20": ("sbuf", [128, 20], "float32"), "j832": ("sbuf", [128, 20], "float32"),
    "hm0": ("sbuf", [128, 640], "float32"), "hs0": ("sbuf", [128, 640], "float32"),
    "hm1": ("sbuf", [128, 640], "float32"), "hs1": ("sbuf", [128, 640], "float32"),
    "ph": ("sbuf", [128, 52], "float32"), "pe": ("sbuf", [128, 40], "float32"), "lt": ("sbuf", [128, 20], "float32"), "rt": ("sbuf", [128, 20], "float32"),
    "w1": ("sbuf", [128, 26], "float32"), "w2": ("sbuf", [128, 26], "float32"), "w3": ("sbuf", [128, 26], "float32"), "w4": ("sbuf", [128, 26], "float32"),
    "bA": ("sbuf", [128, 92], "float32"), "mL": ("sbuf", [128, 92], "float32"), "mR": ("sbuf", [128, 92], "float32"),
    "g1": ("sbuf", [128, 72], "float32"), "g2": ("sbuf", [128, 72], "float32"), "g3": ("sbuf", [128, 72], "float32"),
    "ta": ("sbuf", [128, 92], "float32"), "tb": ("sbuf", [128, 92], "float32"), "tq": ("sbuf", [128, 92], "float32"), "tw": ("sbuf", [128, 20], "float32"), "te": ("sbuf", [128, 20], "float32"),
    "oA": ("sbuf", [128, 72], "uint16"), "oB": ("sbuf", [128, 20], "uint16"), "l4": ("sbuf", [128, 80], "uint16"),
    "tab": ("sbuf", [128, 1152], "float32"),
    "bm": ("sbuf", [128, 2 * HALF], "float32"), "bs": ("sbuf", [128, 2 * HALF], "float32"),
    "cm": ("sbuf", [128, 48], "float32"), "cs": ("sbuf", [128, 48], "float32"), "acs": ("sbuf", [128, 4], "float32"),
    "ew": ("sbuf", [128, 516], "bfloat16"), "e1": ("sbuf", [128, 516], "bfloat16"), "e32": ("sbuf", [128, 516], "bfloat16"),
    "qe": ("sbuf", [128, 1024], "float8_e4m3fn_x4"), "se": ("sbuf", [128, 1024], "uint8"),
    "ct": ("sbuf", [128, 512], "bfloat16"), "qc": ("sbuf", [128, 128], "float8_e4m3fn_x4"), "sct": ("sbuf", [128, 128], "uint8"),
    "ft": ("sbuf", [128, 512], "bfloat16"), "qf": ("sbuf", [128, 128], "float8_e4m3fn_x4"), "sf": ("sbuf", [128, 128], "uint8"),
    "ut": ("sbuf", [128, 512], "bfloat16"), "qu": ("sbuf", [128, 128], "float8_e4m3fn_x4"), "su": ("sbuf", [128, 128], "uint8"),
    "qu2": ("sbuf", [128, 128], "float8_e4m3fn_x4"), "su2": ("sbuf", [128, 128], "uint8"),
    "vt": ("sbuf", [128, 512], "bfloat16"), "qv": ("sbuf", [128, 128], "float8_e4m3fn_x4"), "sv": ("sbuf", [128, 128], "uint8"),
    "wq": ("sbuf", [128, 512], "float8_e4m3fn_x4"), "wsb": ("sbuf", [128, 512], "uint8"),
    "qx": ("sbuf", [128, NC], "float8_e4m3fn_x4"), "sx": ("sbuf", [128, NC], "uint8"),
    "gr": ("sbuf", [128, 4 * HALF], "bfloat16"), "q1": ("sbuf", [128, HALF], "float8_e4m3fn_x4"), "s1": ("sbuf", [128, HALF], "uint8"),
    "gt": ("sbuf", [128, 4 * HALF], "bfloat16"), "q2": ("sbuf", [128, HALF], "float8_e4m3fn_x4"), "s2": ("sbuf", [128, HALF], "uint8"),
    "ow": ("sbuf", [128, 4 * HALF], "bfloat16"), "qo": ("sbuf", [128, HALF], "float8_e4m3fn_x4"), "so": ("sbuf", [128, HALF], "uint8"),
    "zo": ("sbuf", [128, 4 * HALF], "bfloat16"), "zg": ("sbuf", [128, 4 * HALF], "bfloat16"),
    "qzo": ("sbuf", [128, HALF], "float8_e4m3fn_x4"), "szo": ("sbuf", [128, HALF], "uint8"),
    "qzg": ("sbuf", [128, HALF], "float8_e4m3fn_x4"), "szg": ("sbuf", [128, HALF], "uint8"),
    "yt": ("sbuf", [128, NC], "float32"),
}
for _r in range(3):
    SCRATCH["lc%d" % _r] = ("sbuf", [128, HALF], "float8_e4m3fn_x4")
    SCRATCH["ls%d" % _r] = ("sbuf", [128, HALF], "uint8")
for _b in range(8):
    SCRATCH["ps%d" % _b] = ("psum", [128, 512], "float32")
SEMAPHORES = ["cV", "cS", "cT", "cG", "dX", "dR", "dQ", "dH", "dU", "dV", "dW", "shO", "shG", "dL", "dE", "dOut", "arr0", "arr1", "arr2", "sent"]


def shifts(lo, hi):
    out = []

    def piece(p0, p1, q0):
        slot = q0 // GRP - p0 // GRP + 7
        out.append((p0, p1, q0, 4 * (NC * slot + lo), 4 * (hi - lo)))
    for m in (1, 2):
        k = GRP * m
        piece(0, 128 - k, k)
        piece(128 - k, 128, 0)
        piece(k, 128, 0)
        piece(0, k, 128 - k)
    for grp in (1, 3, 5, 7):
        for d in (3, -3):
            piece(GRP * grp, GRP * grp + GRP, GRP * ((grp + d) % 8))
    return out


def rank_program(g, core, T, topo):
    rank = T.rank_of(core)
    if rank is None:
        return
    eng = {"V": g.vector, "S": g.scalar, "T": g.tensor, "G": g, "Y": g.sync}
    own_sem = {"V": "cV", "S": "cS", "T": "cT", "G": "cG"}
    total = {s: 0 for s in SEMAPHORES}
    local = ("dX", "dR", "dQ", "dH", "dU", "dV", "dW", "shO", "shG", "dL", "dE", "dOut")
    known = {e: {} for e in eng}
    writer, reader = {}, {}

    def gate(e, r, w):
        need = []
        for t in r:
            need += writer.get(t, [])
        for t in w:
            need += writer.get(t, [])
            need += [x for x in reader.get(t, []) if x[3] != e]
        best = {}
        for sem, val, clk, _ in need:
            v = total[sem] if sem in local else val
            best[sem] = max(best.get(sem, 0), v)
        clks = {}
        for sem, val, clk, _ in need:
            for s, v in clk.items():
                if s != sem and s not in local:
                    clks.setdefault(s, []).append((sem, v))
        for sem in best:
            v = best[sem]
            if known[e].get(sem, 0) >= v:
                continue
            if any(o != sem and o in best and x >= v for o, x in clks.get(sem, [])):
                continue
            eng[e].wait_ge(T.sem[sem], v)
        for sem, val, clk, _ in need:
            for s, v in clk.items():
                known[e][s] = max(known[e].get(s, 0), v)
        for sem in best:
            known[e][sem] = max(known[e].get(sem, 0), best[sem])

    def mark(e, sem, val, r, w):
        clk = dict(known[e])
        clk[sem] = val
        x = (sem, val, clk, e)
        for t in w:
            writer[t] = [x]
            reader[t] = []
        for t in r:
            reader.setdefault(t, []).append(x)

    def op(e, call, r, w):
        gate(e, r, w)
        s = own_sem[e]
        total[s] += 1
        call().then_inc(T.sem[s], 1)
        mark(e, s, total[s], r, w)

    def dma(e, sem, out, in_, r, w):
        if sem not in ("shO", "shG"):
            gate(e, r, w)
        total[sem] += 16
        eng[e].dma_start(out, in_).then_inc(T.sem[sem], 16)
        mark(e, sem, total[sem], r, w)

    def ts(out, in0, s1, o1, r, w, s2=None, o2=None):
        if o2 is None:
            op("V", lambda: g.vector.tensor_scalar(out, in0, s1, None, o1), r, w)
        else:
            op("V", lambda: g.vector.tensor_scalar(out, in0, s1, s2, o1, o2), r, w)

    def tt(out, in0, in1, o, r, w):
        op("V", lambda: g.vector.tensor_tensor(out, in0, in1, o), r, w)

    def cp(out, in_, r, w):
        op("V", lambda: g.vector.tensor_copy(out, in_), r, w)

    def fill(ap, c, w):
        op("V", lambda: g.vector.memset(ap, c), (), w)

    def act(out, in_, r, w, scale=1.0, bias=None, fn=None):
        if bias is None:
            op("S", lambda: g.scalar.activation(out, in_, fn or FN.Copy, scale=scale), r, w)
        else:
            op("S", lambda: g.scalar.activation(out, in_, fn or FN.Identity, bias=bias, scale=scale), r, w)

    def scan(out, k, d, r, w):
        op("V", lambda: g.vector.tensor_tensor_scan(out, k, d, 0.0, OP.mult, OP.add), r, w)

    def quant(q, s, a, b, tile, c0, r, w):
        op("V", lambda: g.vector.quantize_mx(q[:, a:b], s[:, a:b], tile[:, c0:c0 + 4 * (b - a)]), r, w)

    def mm(out, l, ls, la, m, ms, ma, n, r, w, start=True, stop=True):
        op("T", lambda: g.tensor.matmul_mx(out, l[:, la:la + 128], ls[:, la:la + 128], m[:, ma:ma + n], ms[:, ma:ma + n], start, stop), r, w)

    def evac(e, out, in_, r, w, scale):
        if e == "S":
            act(out, in_, r, w, scale=scale)
        elif scale == 1.0:
            cp(out, in_, r, w)
        else:
            ts(out, in_, scale, OP.mult, r, w)

    ps = [T["ps%d" % b] for b in range(8)]
    sc = lambda k: T.sc[:, k:k + 1]
    NSH = len(shifts(0, NC))

    def ring(q, sem, k, p0, p1, q0, tok):
        dma(q, sem, T.ri[p0:p1, 26 * k:26 * k + 26], T.ring[q0:q0 + p1 - p0, :], (), (tok,))
    for f in (1, 3, 5, 7):
        ring("S", "dR", 3, GRP * f, GRP * f + GRP, GRP * f, ("l1", f))
        e = (f + 1) % 8
        ring("Y", "dR", 3, GRP * e, GRP * e + GRP, GRP * f, ("l1", e))
    ring("S", "dR", 4, 0, 128 - GRP, GRP, "l2a")
    ring("Y", "dR", 4, 128 - GRP, 128, 0, "l2b")
    dma("Y", "dX", T.win[:, 4 * CEN:4 * (CEN + NC)], T.x[:, :], (), ("xO", "xG"))
    dma("Y", "dU", T.ut[:, :], T.u[:, :], (), ("ut",))
    n = 0
    for k, src in ((0, -1), (1, 1)):
        for h in range(8):
            f = (h // 2 * 2 + src) % 8
            ring("SY"[n % 2], "dQ", k, GRP * h, GRP * h + GRP, GRP * f, ("q", k, h))
            n += 1
    ring("S", "dQ", 2, 0, 128 - 2 * GRP, 2 * GRP, "l3a")
    ring("Y", "dQ", 2, 128 - 2 * GRP, 128, 0, "l3b")
    qtok = tuple(("q", k, h) for k in range(2) for h in range(8)) + ("l3a", "l3b")

    fl = dict(allow_small_or_imprecise_dtypes=True)
    op("G", lambda: g.iota(T.pI[:, :], [[0, 8]], 0, 1), (), ("pI",))
    op("G", lambda: g.iota(T.idt[:, 0:RING], [[1, RING]], 0, 0, **fl), (), ("id0",))
    op("G", lambda: g.iota(T.j20[:, :], [[16, 20]], 0, 1, **fl), (), ("j20",))
    op("G", lambda: g.iota(T.jm[:, :], [[0, 40], [1, 16]], 0, 0, **fl), (), ("jm",))
    op("G", lambda: g.iota(T.jj[:, 0:40], [[1, 5], [1, 8]], 63, 0), (), ("jja",))
    op("G", lambda: g.iota(T.jj[:, 40:48], [[1, 8]], 64, 0), (), ("jjb",))
    op("G", lambda: g.iota(T.idt[:, RING:2560], [[1, 2560 - RING]], RING, 0, **fl), (), ("id1",))
    op("G", lambda: g.iota(T.ew[:, :], [[0, 516]], 32, 0, **fl), (), ("ew",))
    op("G", lambda: g.affine_select(T.e1[:, :], T.ew[:, :], [[1, 516]], OP.is_equal, 0.0, -3, -4), ("ew",), ("e1",))
    ts(T.gI[:, :], T.pI[:, :], 4, OP.arith_shift_right, ("pI",), ("gI",))
    ts(T.kI[:, :], T.pI[:, :], 15, OP.bitwise_and, ("pI",), ("kI",))
    ts(T.p7[:, :], T.pI[:, :], 7, OP.bitwise_and, ("pI",), ("p7",))
    ts(T.pr[:, :], T.gI[:, :], 1, OP.bitwise_and, ("gI",), ("pr",))
    gc, pc = T.gI[:, 0:1], T.pr[:, 0:1]
    ts(sc(2), gc, -320.0, OP.mult, ("gI",), ("s2",), float(CEN), OP.add)
    ts(sc(15), gc, 304.0, OP.mult, ("gI",), ("s15",))
    ts(sc(19), T.kI[:, 0:1], -1.0, OP.mult, ("kI",), ("s19",))
    ts(sc(20), pc, float(DBL), OP.mult, ("pr",), ("s20",), 320.0, OP.add)
    ts(sc(21), pc, -float(DBL + 320), OP.mult, ("pr",), ("s21",), float(DBL + 320), OP.add)
    ts(sc(24), pc, float(INV), OP.mult, ("pr",), ("s24",))
    ts(T.kl[:, 0:20], T.j20[:, :], sc(15), OP.add, ("j20", "s15"), ("kl0",))
    tt(sc(14), sc(2), sc(24), OP.add, ("s2", "s24"), ("s14",))
    tt(sc(16), sc(15), sc(24), OP.add, ("s15", "s24"), ("s16",))
    ts(sc(7), sc(2), 4.0, OP.mult, ("s2",), ("s7",))
    ts(T.kl[:, 20:40], T.j20[:, :], sc(16), OP.add, ("j20", "s16"), ("kl1",))
    cp(sc(0), gc, ("gI",), ("s0",))
    cp(sc(1), pc, ("pr",), ("s1",))
    ts(sc(4), gc, -16.0, OP.mult, ("gI",), ("s4",), float(CEN), OP.add)
    ts(sc(5), gc, 7.0, OP.is_equal, ("gI",), ("s5",), -2560.0, OP.mult)
    ts(sc(6), pc, float(INV + NC), OP.mult, ("pr",), ("s6",))
    ts(sc(8), pc, 320.0, OP.mult, ("pr",), ("s8",))
    tt(sc(9), sc(4), sc(5), OP.add, ("s4", "s5"), ("s9",))
    ts(sc(12), gc, -16.0, OP.mult, ("gI",), ("s12",), 832.0, OP.add)
    ts(sc(22), gc, 0.0, OP.is_equal, ("gI",), ("s22",), -2560.0, OP.mult)
    tt(sc(17), sc(9), sc(6), OP.add, ("s9", "s6"), ("s17",))
    ts(sc(23), pc, -10000.0, OP.mult, ("pr",), ("s23",), 10001.0, OP.add)
    ts(sc(25), sc(22), -416.0, OP.add, ("s22",), ("s25",))
    tt(sc(18), sc(17), sc(8), OP.add, ("s17", "s8"), ("s18",))
    ts(T.ul[:, :], T.p7[:, :], 16, OP.mult, ("p7",), ("ul",))
    for h in (0, 2, 4, 6):
        dma("Y", "dH", T.kl[GRP * h:GRP * h + GRP, 0:26], T.ring[GRP * h:GRP * h + GRP, :], ("kl0", "kl1"), (("kh", h),))
    klt = ("kl0", "kl1") + tuple(("kh", h) for h in (0, 2, 4, 6))
    for k, (p0, p1, q0, c, n) in enumerate(shifts(0, NC)):
        dma("Y", "shG", T.win[p0:p1, c:c + n], T.x[q0:q0 + p1 - p0, :], (), (("shG", k),))
    dma("Y", "dW", T.wq[:, :].bitcast(dt.uint8), T.wc[:, :], (), ("wq",))
    dma("Y", "dW", T.wsb[:, :], T.ws[:, :], (), ("wsb",))
    dma("Y", "dV", T.vt[:, :], T.v[:, :], (), ("vt",))
    act(T.iv1[:, :], T.idt[:, 0:RING], ("id0", "s20"), ("iv1",), bias=sc(20))
    act(T.map[:, CEN:CEN + NC], T.idt[:, 0:NC], ("id0",), ("map0",), bias=float(IDB + CEN))
    for k, c in enumerate((INV + CEN, INV + CEN + 2 * NC, INV + NC)):
        act(T.map[:, c:c + NC], T.idt[:, 0:NC], ("id0",), ("map%d" % (k + 1),), scale=0.0, bias=float(ABS))
    act(T.iv2[:, :], T.idt[:, 0:RING], ("id0", "s21"), ("iv2",), bias=sc(21))
    act(T.jd[:, :], T.jm[:, :], ("jm", "s19"), ("jd",), bias=sc(19), fn=FN.Abs)
    act(T.mask[:, :], T.jd[:, :], ("jd",), ("mask",), scale=-1.0, bias=1.0, fn=FN.Relu)
    act(T.keep[:, :], T.jm[:, :], ("jm",), ("keep",), fn=FN.Sign)
    mapt = tuple("map%d" % k for k in range(4))
    for k, (p0, p1, t, c) in enumerate(((0, 128, 0, 1.0), (0, 128, 1, 1.0), (0, 64, 2, 0.0), (64, 128, 2, 1.0), (0, 128, 3, 0.0))):
        act(T.ct[p0:p1, t:512:4], T.idt[p0:p1, 0:128], ("id0",), (("ct", k),), scale=0.0, bias=c)
    act(T.ft[:, :], T.jm[:, 0:512], ("jm",), ("ft0", "ft1", "ft2"), scale=0.0)
    fill(T.cst[:, 0:24], -1, ("c0",))
    fill(T.cst[:, 24:32], 3, ("c1",))
    fill(T.cst[:, 32:40], 5, ("c2",))
    fill(T.cst[:, 40:48], 0, ("c3",))

    l1t = tuple(("l1", h) for h in range(8)) + ("l2a", "l2b")
    ts(T.xu[:, 0:26], T.ri[:, 78:104], sc(2), OP.add, l1t + ("s2",), ("xu0",))
    ts(T.xu[:, 26:52], T.ri[:, 104:130], sc(14), OP.add, l1t + ("s14",), ("xu1",))

    def scatter(k, nm):
        op("V", lambda: g.vector.tensor_copy(T.map[:, 0:2 * WINC].indirect(T.xu[:, 26 * k:26 * k + 26]), T[nm][:, :]), (nm, "xu%d" % k), mapt)
    scatter(0, "iv1")
    cp(T.eu[:, :], T.ri[:, 0:78], qtok, ("eu",))
    quant(T.qu, T.su, 0, 128, T.ut, 0, ("ut",), ("qu",))
    scatter(1, "iv2")
    quant(T.qx, T.sx, 0, NC, T.win, 4 * CEN, ("xO", "xG"), ("qxO", "qxG"))
    op("V", lambda: g.vector.tensor_copy(T.qu2[:, 0:128].bitcast(dt.uint32), T.qu[:, 0:128].bitcast(dt.uint32).indirect(T.ul[:, 0:8])), ("qu", "ul"), ("qu2",))
    op("V", lambda: g.vector.tensor_copy(T.su2[:, 0:128], T.su[:, 0:128].indirect(T.ul[:, 0:8])), ("qu", "ul"), ("su2",))
    ts(T.xk[:, :], T.kl[:, :], sc(2), OP.add, klt + ("s2",), ("xk",))
    ts(T.xe[:, 0:20], T.j20[:, :], sc(17), OP.add, ("j20", "s17"), ("xe0",))
    ts(T.xe[:, 20:40], T.j20[:, :], sc(18), OP.add, ("j20", "s18"), ("xe1",))
    act(T.src[:, IDB + CEN - NC:IDB + CEN + 2 * NC], T.idt[:, 0:960], ("id0", "id1"), ("src0",), scale=4.0, bias=float(4 * (CEN - NC)))
    act(T.src[:, IDB:IDB + NC], T.idt[:, 0:NC], ("id0",), ("src1",), scale=4.0)
    for k in range(3):
        act(T.src[:, DBL * k:DBL * k + 320], T.idt[:, 0:2560].indirect(T.eu[:, 26 * k + 6:26 * k + 26]), ("id0", "id1", "eu", "s7"), (("sr", k, 0),), scale=4.0, bias=sc(7))
        act(T.src[:, DBL * k + 320:DBL * k + 736], T.idt[:, 0:2560].indirect(T.eu[:, 26 * k:26 * k + 26]), ("id0", "id1", "eu", "s7"), (("sr", k, 1),), scale=4.0, bias=sc(7))
    srct = ("src0", "src1") + tuple(("sr", k, i) for k in range(3) for i in range(2))

    def look(k, off, r):
        m, s = T["hm%d" % k], T["hs%d" % k]
        tt(m[:, :], T.map[:, 0:2 * WINC].indirect(off), T.mask[:, :], OP.mult, mapt + ("mask",) + r, (("hm", k),))
        scan(s[:, :], T.keep[:, :], m[:, :], ("keep", ("hm", k)), (("hs", k),))

    def compare(t):
        ts(T.ft[:, t:192:4], ps[t][:, 0:48], 0.0, OP.is_gt, (("ps", t),), ("ft%d" % t,))

    def counts_a():
        mm(ps[0][:, 0:128], T.qx, T.sx, 192, T.qu2, T.su2, 0, 128, ("qxO", "qu2", "su2"), (("ps", 0),))

    def counts_b():
        mm(ps[1][:, 0:128], T.qx, T.sx, 0, T.qu2, T.su2, 0, 128, ("qxG", "qu2", "su2"), (("ps", 1),))
        mm(ps[2][:, 0:128], T.qx, T.sx, 64, T.qu2, T.su2, 0, 128, ("qxO", "qxG", "qu2", "su2"), (("ps", 2),))
        for t in range(3):
            compare(t)
        quant(T.qf, T.sf, 0, 128, T.ft, 0, ("ft0", "ft1", "ft2"), ("qf",))
        mm(ps[3][:, 0:128], T.qc, T.sct, 0, T.qf, T.sf, 0, 128, ("qc", "qf"), (("ps", 3),))

    def counts_c():
        tt(T.cm[:, :], ps[3][:, 0:48], T.mk[:, :], OP.mult, (("ps", 3), "mk"), ("cm",))
        scan(T.cs[:, :], T.kp8[:, :], T.cm[:, :], ("cm", "kp8"), ("cs",))

    counts_a()
    look(0, T.xk[:, :], ("xk",))
    fill(T.kp8[:, :], 1.0, ("kp8",))
    fill(T.bA[:, :], float(IDB + CEN), ("bA0", "bA1", "bA2", "bA3"))
    h0 = ("hs", 0)
    ts(T.w1[:, :], T.hs0[:, 15:RING:16], float(IDB), OP.is_ge, (h0,), ("w1",), -320.0, OP.mult)
    ts(T.w2[:, :], T.hs0[:, 15:RING:16], float(IDB), OP.is_ge, (h0, "s25"), ("w2",), sc(25), OP.mult)
    ts(T.w3[:, :], T.hs0[:, 15:RING:16], float(DBL), OP.add, (h0,), ("w3",))
    tt(T.ph[:, 0:26], T.hs0[:, 15:RING:16], T.w1[:, :], OP.add, (h0, "w1"), ("ph0",))
    tt(T.ph[:, 26:52], T.w3[:, :], T.w2[:, :], OP.add, ("w3", "w2"), ("ph1",))
    cp(T.bA[:, 0:20], T.hs0[:, 15:NC:16], (h0,), ("bA0",))
    cp(T.bA[:, 20:46], T.hs0[:, 15:RING:16], (h0,), ("bA1",))
    for k, h in enumerate((1, 3, 5, 7)):
        f = (h + 1) % 8
        dma("Y", "dL", T.bA[GRP * h:GRP * h + GRP, 20:46], T.ph[GRP * (h - 1):GRP * h, 0:26], ("ph0", "bA1"), (("bh", k),))
        dma("Y", "dL", T.bA[GRP * h:GRP * h + GRP, 46:72], T.ph[GRP * f:GRP * f + GRP, 26:52], ("ph1", "bA2"), (("bh", 4 + k),))
    ts(T.rt[:, :], T.hs0[:, NC + 15:640:16], 2.0, OP.mult, (h0, "s23"), ("rt",), sc(23), OP.add)
    look(1, T.xe[:, :], ("xe0", "xe1"))
    fill(T.kp8[:, 0:48:8], 0.0, ("kp8",))
    quant(T.qc, T.sct, 0, 128, T.ct, 0, tuple(("ct", k) for k in range(5)), ("qc",))
    ts(T.pe[:, :], T.hs1[:, 15:640:16], 2.0, OP.mult, (("hs", 1),), ("pe",))
    for k, h in enumerate((1, 3, 5, 7)):
        e, f = (h + 1) % 8, (h + 2) % 8
        dma("Y", "dE", T.lt[GRP * e:GRP * e + GRP, :], T.pe[GRP * h:GRP * h + GRP, 0:20], ("pe",), (("lt", k),))
        dma("Y", "dE", T.lt[GRP * f:GRP * f + GRP, :], T.pe[GRP * h:GRP * h + GRP, 20:40], ("pe",), (("lt", 4 + k),))
    counts_b()
    ts(T.cst[:, :], T.cst[:, :], sc(1), OP.mult, ("c0", "c1", "c2", "c3", "s1"), ("c0",))
    ts(T.j832[:, :], T.j20[:, :], sc(12), OP.add, ("j20", "s12"), ("j832",))
    tt(T.jj[:, :], T.jj[:, :], T.cst[:, :], OP.subtract, ("jja", "jjb", "c0"), ("jja",))
    tt(T.te[:, :], T.rt[:, :], T.j832[:, :], OP.min, ("rt", "j832"), ("te",))
    ts(T.jj[:, :], T.jj[:, :], sc(0), OP.subtract, ("jja", "s0"), ("jja",))
    ts(T.mR[:, 72:92], T.rt[:, :], 832.0, OP.is_lt, ("rt",), ("mE",), 2.0, OP.mult)
    ts(T.jj[:, :], T.jj[:, :], 7, OP.bitwise_and, ("jja",), ("jja",))
    for b in range(2):
        quant(T.qe, T.se, 128 * b, 128 * b + 128, T.e1, 3 - b, ("e1",), (("qe", b),))
    ts(T.mk[:, :], T.jj[:, :], 0.0, OP.is_equal, ("jja",), ("mk",))
    for b in range(2, 4):
        quant(T.qe, T.se, 128 * b, 128 * b + 128, T.e1, 3 - b, ("e1",), (("qe", b),))
    bAt = ("bA0", "bA1", "bA2") + tuple(("bh", k) for k in range(8))
    ts(T.g1[:, :], T.bA[:, 0:72], float(DBL), OP.is_ge, bAt, ("g1",))
    ts(T.g2[:, :], T.bA[:, 0:72], float(2 * DBL), OP.is_ge, bAt, ("g2",))
    ts(T.g3[:, :], T.bA[:, 0:72], float(3 * DBL), OP.is_ge, bAt, ("g3",))
    ts(T.mR[:, 20:46], T.bA[:, 20:46], float(DBL), OP.is_lt, bAt, ("mA",))
    tt(T.mL[:, 0:72], T.g1[:, :], T.g2[:, :], OP.subtract, ("g1", "g2"), ("mB",))
    tt(T.mR[:, 46:72], T.g2[:, 46:72], T.g3[:, 46:72], OP.subtract, ("g2", "g3"), ("mC",))
    ltt = tuple(("lt", k) for k in range(8))

    cs = lambda k: T.cs[:, 8 * k + 7:8 * k + 8]

    def lists():
        ts(T.ta[:, 0:72], T.mL[:, 0:72], cs(0), OP.mult, ("mB", "cs"), ("ta0",))
        act(T.tb[:, 46:72], T.mR[:, 46:72], ("mC", "cs"), ("tb1",), scale=cs(4))
        act(T.tb[:, 72:92], T.mR[:, 72:92], ("mE", "cs"), ("tb2",), scale=cs(3))
        ts(T.ta[:, 72:92], T.mL[:, 72:92], cs(1), OP.mult, ("mD", "cs"), ("ta1",))
        ts(T.tb[:, 20:46], T.mR[:, 20:46], cs(2), OP.mult, ("mA", "cs"), ("tb0",))
        tt(T.tq[:, :], T.bA[:, :], T.ta[:, :], OP.subtract, bAt + ("bA3", "ta0", "ta1"), ("tq",))
        tt(T.tq[:, 20:92], T.tq[:, 20:92], T.tb[:, 20:92], OP.subtract, ("tq", "tb0", "tb1", "tb2"), ("tq",))
        cp(T.oA[:, :], T.tq[:, 0:72], ("tq",), ("oA",))
        act(T.tab[:, 0:832:2], T.src[:, :].indirect(T.oA[:, 20:46]), srct + ("oA",), ("tab0",))
        act(T.tab[:, 1:512:2], T.src[:, :].indirect(T.oA[:, 46:62]), srct + ("oA",), ("tab1",))
        ts(T.tw[:, :], T.tq[:, 72:92], 0.0, OP.is_lt, ("tq",), ("tw",), 832.0, OP.mult)
        cp(T.tab[:, 832:1152], T.src[:, :].indirect(T.oA[:, 0:20]), srct + ("oA",), ("tab2",))
        cp(T.tab[:, 513:832:2], T.src[:, :].indirect(T.oA[:, 62:72]), srct + ("oA",), ("tab3",))
        tt(T.tw[:, :], T.tq[:, 72:92], T.tw[:, :], OP.add, ("tq", "tw"), ("tw",))
        cp(T.oB[:, :], T.tw[:, :], ("tw",), ("oB",))

    def pick(h):
        tt(T.bm[:, HALF * h:HALF * h + HALF], T.tab[:, :].indirect(T.oB[:, 10 * h:10 * h + 10]), T.mask[:, 0:HALF], OP.mult, ("tab0", "tab1", "tab2", "tab3", "oB", "mask"), (("bm", h),))

    def fold(h):
        scan(T.bs[:, HALF * h:HALF * h + HALF], T.keep[:, 0:HALF], T.bm[:, HALF * h:HALF * h + HALF], ("keep", ("bm", h)), (("bs", h),))

    def offsets(h):
        for t in (2, 0, 3, 1):
            c = 40 * h + 10 * t
            ts(T.l4[:, c:c + 10], T.bs[:, HALF * h + 15:HALF * h + HALF:16], float(t), OP.add, (("bs", h),), (("l4", h, t),))

    def gather(h, tile, tok):
        wt = ("xO", "xG") + tuple((n, k) for n in ("shO", "shG") for k in range(NSH))
        for t in (2, 0, 3, 1):
            c = 40 * h + 10 * t
            src = T.win[:, :].indirect(T.l4[:, c:c + 10])
            if t >= 2:
                act(tile[:, t:4 * HALF:4], src, wt + (("l4", h, t),), ((tok, t),))
            else:
                cp(tile[:, t:4 * HALF:4], src, wt + (("l4", h, t),), ((tok, t),))

    def unpack(q, s, qt, base, tile, tok, beside=()):
        for b in range(4):
            mm(ps[base + b][:, 0:HALF], T.qe, T.se, 128 * b, q, s, 0, HALF, (("qe", b),) + qt, (("ps", base + b),))
        for b in range(4):
            if b % 2 == 0 and beside:
                beside[b // 2]()
            evac("VS"[b % 2], tile[:, b:4 * HALF:4], ps[base + b][:, 0:HALF], (("ps", base + b),), ((tok, b),), 2.0 ** -5)
        if beside:
            beside[2]()

    def first(base, q, s, qt):
        for b in range(4):
            mm(ps[base + b][:, 0:HALF], T.qe, T.se, 128 * b, q, s, 0, HALF, (("qe", b),) + qt, (("ps", base + b),), True, False)

    def layer(base, q, s, qt, c0, tok):
        for b in range(4):
            mm(ps[base + b][:, 0:HALF], T.wq, T.wsb, 128 * b, q, s, 0, HALF, ("wq", "wsb") + qt, (("ps", base + b),), False, True)
        for b in range(4):
            evac("VS"[b % 2], T.win[:, c0 + b:c0 + 4 * HALF:4], ps[base + b][:, 0:HALF], (("ps", base + b),), ((tok, b),), 2.0 ** -5)

    four = lambda t: tuple((t, b) for b in range(4))

    for rd in range(3):
        last = rd == 2
        counts_c()
        if rd == 0:
            ts(T.mL[:, 72:92], T.lt[:, :], 832.0, OP.is_lt, ltt, ("mD",), 2.0, OP.mult)
            tt(T.bA[:, 72:92], T.lt[:, :], T.te[:, :], OP.min, ltt + ("te",), ("bA3",))
        lists()
        pick(0)
        fold(0)
        offsets(0)
        gather(0, T.gr, "gr")
        quant(T.q1, T.s1, 0, HALF, T.gr, 0, four("gr"), ("q1",))
        unpack(T.q1, T.s1, ("q1",), 4, T.gt, "gt", (lambda: pick(1), lambda: fold(1), lambda: offsets(1)))
        quant(T.q2, T.s2, 0, HALF, T.gt, 0, four("gt"), ("q2",))
        dst = T.cores[rank ^ MASKS[rd]]
        rid, pid = topo.addr(dst)[0], topo.addr(dst)[1]
        ne, mask = len(topo.engines(core, dst)), topo.mask(core, dst)
        arr = "arr%d" % rd
        gate("G", ("q2",), ())
        g.remote_dma(T["lc%d" % rd][:, :].bitcast(dt.uint8), T.q2[:, :].bitcast(dt.uint8), T.sem[arr], T.sem.sent, pid, rid, mask)
        g.remote_dma(T["ls%d" % rd][:, :], T.s2[:, :], T.sem[arr], T.sem.sent, pid, rid, mask)
        total["sent"] += 2 * ne
        total[arr] += 2 * ne
        mark("G", "sent", total["sent"], ("q2",), ())
        land = ("land", rd)
        writer[land] = [(arr, 2 * ne, {}, "R")]
        gather(1, T.ow, "ow")
        quant(T.qo, T.so, 0, HALF, T.ow, 0, four("ow"), ("qo",))
        unpack(T.qo, T.so, ("qo",), 0, T.zo, "zo")
        first(0, T.qo, T.so, ("qo",))
        quant(T.qzo, T.szo, 0, HALF, T.zo, 0, four("zo"), ("qzo",))
        layer(0, T.qzo, T.szo, ("qzo",), 4 * (CEN + HALF), "xo")
        writer["xO"], reader["xO"] = sum([writer[("xo", b)] for b in range(4)], []), []
        if not last:
            gate("Y", ("xO",), tuple(("shO", k) for k in range(NSH)))
            for k, (p0, p1, q0, c, n) in enumerate(shifts(HALF, NC)):
                dma("Y", "shO", T.win[p0:p1, c:c + n], T.win[q0:q0 + p1 - p0, 4 * (CEN + HALF):4 * (CEN + NC)], ("xO",), (("shO", k),))
        unpack(T["lc%d" % rd], T["ls%d" % rd], (land,), 4, T.zg, "zg")
        first(4, T["lc%d" % rd], T["ls%d" % rd], (land,))
        quant(T.qzg, T.szg, 0, HALF, T.zg, 0, four("zg"), ("qzg",))
        quant(T.qx, T.sx, HALF, NC, T.win, 4 * (CEN + HALF), ("xO",), ("qxO",))
        act(T.acs[:, rd:rd + 1], cs(5), ("cs",), (("ac", rd),))
        if rd == 0:
            quant(T.qv, T.sv, 0, 128, T.vt, 0, ("vt",), ("qv",))
        layer(4, T.qzg, T.szg, ("qzg",), 4 * CEN, "xg")
        writer["xG"], reader["xG"] = sum([writer[("xg", b)] for b in range(4)], []), []
        if last:
            dma("Y", "dOut", T.oc[:, 4 * HALF:4 * NC], T.qx[:, HALF:NC].bitcast(dt.uint8), ("qxO",), ("oco",))
            for k in range(4):
                dma("Y", "dOut", T.osc[4 * k:4 * k + 4, HALF:NC], T.sx[32 * k:32 * k + 4, HALF:NC], ("qxO",), (("oso", k),))
            dma("Y", "dOut", T.ac[:, :], T.acs[0:128:16, 0:3], (("ac", 0), ("ac", 1), ("ac", 2)), ("aco",))
            mm(ps[0][:, 0:HALF], T.qv, T.sv, 0, T.qx, T.sx, HALF, HALF, ("qv", "qxO"), (("ps", 0),))
            act(T.yt[:, HALF:NC], ps[0][:, 0:HALF], (("ps", 0),), ("yO",))
            dma("Y", "dOut", T.y[:, HALF:NC], T.yt[:, HALF:NC], ("yO",), ("you",))
        else:
            counts_a()
        if not last:
            gate("Y", ("xG",), tuple(("shG", k) for k in range(NSH)))
            for k, (p0, p1, q0, c, n) in enumerate(shifts(0, HALF)):
                dma("Y", "shG", T.win[p0:p1, c:c + n], T.win[q0:q0 + p1 - p0, 4 * CEN:4 * (CEN + HALF)], ("xG",), (("shG", k),))
        quant(T.qx, T.sx, 0, HALF, T.win, 4 * CEN, ("xG",), ("qxG",))
        if last:
            dma("Y", "dOut", T.oc[:, 0:4 * HALF], T.qx[:, 0:HALF].bitcast(dt.uint8), ("qxG",), ("ocg",))
            for k in range(4):
                dma("S", "dOut", T.osc[4 * k:4 * k + 4, 0:HALF], T.sx[32 * k:32 * k + 4, 0:HALF], ("qxG",), (("osg", k),))
            mm(ps[1][:, 0:HALF], T.qv, T.sv, 0, T.qx, T.sx, 0, HALF, ("qv", "qxG"), (("ps", 1),))
            cp(T.yt[:, 0:HALF], ps[1][:, 0:HALF], (("ps", 1),), ("yG",))
            dma("Y", "dOut", T.y[:, 0:HALF], T.yt[:, 0:HALF], ("yG",), ("yog",))
        else:
            counts_b()
    for s in SEMAPHORES:
        if total[s] and known["Y"].get(s, 0) < total[s]:
            g.sync.wait_ge(T.sem[s], total[s])
